import numpy as np
import ml_dtypes


def mxq(x, axis, fmt="e4m3"):
    dtype, down = {"e4m3": (ml_dtypes.float8_e4m3fn, 7), "e5m2": (ml_dtypes.float8_e5m2, 14)}[fmt]
    v = np.moveaxis(np.asarray(x, np.float32).astype(ml_dtypes.bfloat16).astype(np.float64), axis, -1)
    blocks = v.reshape(v.shape[:-1] + (-1, 32))
    amax = np.abs(blocks).max(-1, keepdims=True)
    byte = np.maximum(np.where(amax > 0, np.frexp(amax)[1] - 1 + 127, 0) - down, 1)
    scale = np.exp2(byte - 127.0)
    codes = (blocks / scale).astype(np.float32).astype(dtype).astype(np.float64)
    return np.moveaxis((codes * scale).reshape(v.shape), -1, axis)


WIDE = False


def mx_kscale(k):
    if not WIDE:
        return np.ones(k)
    levels = np.array([10, -10, 5, -5, 0])
    if k % 512:
        return np.exp2(np.random.permutation(np.resize(levels, k // 32))).repeat(32)
    a = np.empty((k // 512, 16))
    for p in range(k // 512):
        a[p, :8] = np.random.permutation(np.resize(levels, 8))
        for g in range(8):
            far = levels[np.abs(levels - a[p, g]) >= 10]
            a[p, g + 8] = far[np.random.randint(len(far))]
    return np.exp2(a.ravel()).repeat(32)


BF16 = ml_dtypes.bfloat16


def bf(x):
    return np.asarray(x, np.float32).astype(BF16)


def f64(x):
    return np.asarray(x).astype(np.float64)


E2M1 = np.array([0.0, 0.5, 1.0, 1.5, 2.0, 3.0, 4.0, 6.0, -0.0, -0.5, -1.0, -1.5, -2.0, -3.0, -4.0, -6.0])


def pack_weight(w, fmt):
    k, n = w.shape
    w = f64(bf(w)).reshape(k // 32, 32, n)
    amax = np.abs(w).max(1)
    if fmt == "e4m3":
        byte = np.frexp(amax)[1] - 1 + 127 - 7
    else:
        mant, ex = np.frexp(amax / 6.0)
        byte = np.where(mant > 0.5, ex, ex - 1) + 127
    byte = np.clip(np.where(amax > 0, byte, 1), 1, 254)
    scaled = (w * np.exp2(127.0 - byte)[:, None, :]).reshape(k, n).astype(np.float32)
    by_word = np.ascontiguousarray(scaled.reshape(k // 512, 128, 4, n).transpose(0, 1, 3, 2))
    if fmt == "e4m3":
        words = by_word.astype(ml_dtypes.float8_e4m3fn).view(np.uint8)
    else:
        c = by_word.astype(ml_dtypes.float4_e2m1fn).view(np.uint8) & 0xF
        words = c[..., 0::2] | (c[..., 1::2] << 4)
    return np.ascontiguousarray(words), np.ascontiguousarray(byte.astype(np.uint8).reshape(k // 512, 16, n))


def unpack_weight(words, scales, fmt):
    g, p, n, _ = words.shape
    if fmt == "e4m3":
        vals = np.ascontiguousarray(words).view(ml_dtypes.float8_e4m3fn).astype(np.float64)
    else:
        nib = np.empty((g, p, n, 4), np.uint8)
        nib[..., 0::2] = words & 0xF
        nib[..., 1::2] = words >> 4
        vals = E2M1[nib]
    vals = vals * np.repeat(np.exp2(scales.astype(np.float64) - 127.0), 8, axis=1)[..., None]
    return vals.transpose(0, 1, 3, 2).reshape(g * 512, n)


N, K, P, H = 1024, 1536, 1024, 1024


def draw0():
    s = mx_kscale(K)
    r = mx_kscale(P)
    t = mx_kscale(P)
    z = bf(np.random.standard_normal((N, K)) * s)
    m = bf(np.random.standard_normal((N, P)) * r)
    ez = bf(np.random.standard_normal(K) / np.sqrt(K) / s)
    at_words, at_scales = pack_weight(np.random.standard_normal((P, P)) / np.sqrt(P) / r[:, None] * t, "e4m3")
    bvec = bf(np.random.standard_normal(P) * 0.7 * t)
    wz_words, wz_scales = pack_weight(np.random.standard_normal((K, H)) * 0.7 / np.sqrt(K) / s[:, None], "e4m3")
    wm_words, wm_scales = pack_weight(np.random.standard_normal((P, H)) * 0.7 / np.sqrt(P) / t[:, None], "e4m3")
    return {
        "z": z,
        "m": m,
        "ez": ez,
        "at_words": at_words,
        "at_scales": at_scales,
        "bvec": bvec,
        "wz_words": wz_words,
        "wz_scales": wz_scales,
        "wm_words": wm_words,
        "wm_scales": wm_scales,
    }


def write_scalar(z, ez):
    return np.sum(z * ez[None, :], axis=-1)


def update_memory(m, u, at, bvec):
    a = mxq(m, 1, "e4m3") @ at
    return a + u[:, None] * bvec[None, :]


def core(z, m, ez, at_words, at_scales, bvec, wz_words, wz_scales, wm_words, wm_scales):
    z, m = f64(z), f64(m)
    at = unpack_weight(at_words, at_scales, "e4m3")
    wz = unpack_weight(wz_words, wz_scales, "e4m3")
    wm = unpack_weight(wm_words, wm_scales, "e4m3")
    u = write_scalar(z, f64(ez))
    m_new = update_memory(m, u, at, f64(bvec))
    s = (mxq(z, 1, "e4m3") @ wz) + (mxq(m_new, 1, "e4m3") @ wm)
    return np.tanh(s)


def e4m3fn_bytes(y):
    return np.clip(np.asarray(y, np.float64), -448.0, 448.0).astype(np.float32).astype(ml_dtypes.float8_e4m3fn).view(np.uint8)


def e4m3fn_values(b):
    return np.asarray(b, np.uint8).view(ml_dtypes.float8_e4m3fn).astype(np.float64)


def setup_inputs():
    d = draw0()
    x0 = np.asarray(d['m']).astype(np.float64)
    s = (np.max(np.abs(x0), axis=(0,), keepdims=True) / 448.0).astype(np.float32)
    out = {}
    for k, v in d.items():
        if k == 'm':
            out['m_bytes'] = e4m3fn_bytes(x0 / s.astype(np.float64))
            out['m_scale'] = s
        else:
            out[k] = v
    return out


def reference(z, m_bytes, m_scale, ez, at_words, at_scales, bvec, wz_words, wz_scales, wm_words, wm_scales):
    return core(z, e4m3fn_values(m_bytes) * m_scale.astype(np.float64), ez, at_words, at_scales, bvec, wz_words, wz_scales, wm_words, wm_scales)

@@ -1,0 +1,349 @@
+from contextlib import ExitStack
+
+import concourse.mybir as mybir
+from concourse.masks import make_identity
+
+N, K, P, H = 1024, 1536, 1024, 1024
+FLOPS = 2 * N * H * (K + P) + 2 * N * P * P
+
+F32 = mybir.dt.float32
+BF16 = mybir.dt.bfloat16
+I32 = mybir.dt.int32
+U8 = mybir.dt.uint8
+FP8 = mybir.dt.float8_e4m3fn
+FP8X4 = mybir.dt.float8_e4m3fn_x4
+ACT = mybir.ActivationFunctionType
+ALU = mybir.AluOpType
+
+GZ = 3
+GM = 2
+
+
+def tile_legendrememoryunitstep_w8_kernel(
+    tc, z, m_bytes, m_scale, ez, at_words, at_scales, bvec, wz_words, wz_scales, wm_words, wm_scales, out
+):
+    nc = tc.nc
+    with ExitStack() as ctx:
+        keep = ctx.enter_context(tc.tile_pool(name="keep", bufs=1))
+        stage = ctx.enter_context(tc.tile_pool(name="stage", bufs=8))
+        work = ctx.enter_context(tc.tile_pool(name="work", bufs=3))
+        results = ctx.enter_context(tc.tile_pool(name="results", bufs=4))
+        psum = ctx.enter_context(tc.psum_pool(name="psum", bufs=8))
+        ctx.enter_context(tc.manual_schedule())
+
+        z_rows = z.rearrange("(h p r) k -> h p r k", h=2, p=128)
+        m_rows = m_bytes.rearrange("(h p r) k -> h p (r k)", h=2, p=128)
+        out_rows = out.rearrange("(h p r) c -> h p r c", h=2, p=128)
+
+        ident = keep.tile([128, 128], F32, name="ident")
+        warm = keep.tile([128, 1], F32, name="warm")
+        ez_col = keep.tile([128, GZ, 4], BF16, name="ez_col")
+        b_col = keep.tile([128, GM, 4], BF16, name="b_col")
+        m_fac = keep.tile([128, GM, 4], F32, name="m_fac")
+        m_raw = keep.tile([128, 2, 4096], U8, name="m_raw")
+        at_raw = keep.tile([128, GM, P], I32, name="at_raw", align_bytes=64)
+        at_c = keep.tile([128, GM, P], I32, name="at_c", align_bytes=64)
+        at_sraw = keep.tile([128, P], U8, name="at_sraw", align_bytes=64)
+        at_s = keep.tile([128, P], U8, name="at_s", align_bytes=64)
+        wz_c = keep.tile([128, GZ, H], I32, name="wz_c", align_bytes=64)
+        wz_s = keep.tile([128, H], U8, name="wz_s", align_bytes=64)
+        wm_c = keep.tile([128, GM, H], I32, name="wm_c", align_bytes=64)
+        wm_s = keep.tile([128, H], U8, name="wm_s", align_bytes=64)
+        z_g = keep.tile([128, 2, GZ, 2048], BF16, name="z_g", align_bytes=64)
+        z_c = keep.tile([128, 2, GZ, 512], I32, name="z_c", align_bytes=64)
+        z_s = keep.tile([128, 2, GZ, 512], U8, name="z_s", align_bytes=64)
+        m_g = keep.tile([128, 2, GM, 2048], BF16, name="m_g", align_bytes=64)
+        m_c = keep.tile([128, 2, GM, 512], I32, name="m_c", align_bytes=64)
+        m_s = keep.tile([128, 2, GM, 512], U8, name="m_s", align_bytes=64)
+        u_bc = keep.tile([128, 2, 512], F32, name="u_bc")
+        n_p = keep.tile([128, 2, GM, 4, 512], BF16, name="n_p")
+        n_g = keep.tile([128, 2, GM, 2048], BF16, name="n_g", align_bytes=64)
+        n_c = keep.tile([128, 2, GM, 512], I32, name="n_c", align_bytes=64)
+        n_s = keep.tile([128, 2, GM, 512], U8, name="n_s", align_bytes=64)
+        zin = {}
+        zpre = {}
+        m_bf = {}
+        banks = {}
+
+        def load_z(h, r):
+            zt = stage.tile([128, K], BF16, name="zt")
+            nc.sync.dma_start(out=zt[:], in_=z_rows[h][:, r, :])
+            zin[(h, r)] = zt
+
+        def load_m(h):
+            nc.sync.dma_start(out=m_raw[:, h, :], in_=m_rows[h])
+
+        def load_words(tile, words, g):
+            nc.sync.dma_start(out=tile[:, g, :], in_=words[g].rearrange("p n t -> p (n t)").bitcast(I32))
+
+        def load_scales(tile, scales, groups):
+            for q in range(4):
+                nc.sync.dma_start(
+                    out=tile[32 * q : 32 * q + 4 * groups, :].bitcast(I32),
+                    in_=scales[:, 4 * q : 4 * q + 4, :].bitcast(I32),
+                )
+
+        def pre_z(h, r, engine="v"):
+            zp = stage.tile([128, K // 2], F32, name="zp")
+            copy = nc.vector.tensor_copy if engine == "v" else nc.scalar.copy
+            copy(
+                out=zp[:].rearrange("p (u c) -> p u c", u=2),
+                in_=zin[(h, r)][:].bitcast(F32).rearrange("p (c u) -> p u c", u=2),
+            )
+            zpre[(h, r)] = zp
+
+        def turn_z(h, q, g, direct=False):
+            bank = psum.tile([128, 512], F32, name="bank")
+            for j in range(2):
+                for u in range(2):
+                    if direct:
+                        words = zin[(h, 2 * q + j)][:].bitcast(F32)[:, 256 * g + u : 256 * (g + 1) : 2]
+                    else:
+                        words = zpre[(h, 2 * q + j)][:, u * 384 + g * 128 : u * 384 + (g + 1) * 128]
+                    nc.tensor.transpose(
+                        bank[:, u * 256 + j * 128 : u * 256 + (j + 1) * 128],
+                        words,
+                        ident[:],
+                    )
+            banks[("z", h, q, g)] = bank
+
+        def take_z(h, q, g, engine="s"):
+            bank = banks[("z", h, q, g)]
+            copy = nc.vector.tensor_copy if engine == "v" else nc.scalar.copy
+            copy(
+                out=z_g[:, h, g, q * 1024 : (q + 1) * 1024].bitcast(F32),
+                in_=bank[:].rearrange("p (u c) -> p c u", u=2),
+            )
+
+        def quant(src, codes, scales, h, g):
+            nc.vector.quantize_mx(out=codes[:, h, g, :].bitcast(FP8X4), scales=scales[:, h, g, :], in_=src[:, h, g, :])
+
+        def write_scalar(h, q):
+            bank = psum.tile([128, 512], F32, name="bank")
+            for g in range(GZ):
+                for t in range(4):
+                    nc.tensor.matmul(
+                        bank[:, 0:256],
+                        lhsT=ez_col[:, g, t : t + 1].to_broadcast([128, 128]),
+                        rhs=z_g[:, h, g, q * 1024 : (q + 1) * 1024].rearrange("p (c t) -> p t c", t=4)[:, t, :],
+                        start=(g == 0 and t == 0),
+                        stop=(g == GZ - 1 and t == 3),
+                    )
+            banks[("u", h, q)] = bank
+
+        def take_scalar(h, q, engine="s"):
+            copy = nc.vector.tensor_copy if engine == "v" else nc.scalar.copy
+            copy(out=u_bc[:, h, q * 256 : (q + 1) * 256], in_=banks[("u", h, q)][:, 0:256])
+
+        def cast_m(h, q, engine="s"):
+            mt = work.tile([128, 2048], BF16, name="mt")
+            copy = nc.vector.tensor_copy if engine == "v" else nc.scalar.copy
+            copy(out=mt[:], in_=m_raw[:, h, q * 2048 : (q + 1) * 2048].bitcast(FP8))
+            m_bf[(h, q)] = mt
+
+        def turn_m(h, q, g):
+            bank = psum.tile([128, 512], F32, name="bank")
+            words = m_bf[(h, q)][:].bitcast(F32)
+            for j in range(2):
+                for u in range(2):
+                    lo = 512 * j + 256 * g
+                    nc.tensor.transpose(
+                        bank[:, u * 256 + j * 128 : u * 256 + (j + 1) * 128],
+                        words[:, lo + u : lo + 256 : 2],
+                        ident[:],
+                    )
+            banks[("m", h, q, g)] = bank
+
+        def take_m(h, q, g):
+            bank = banks[("m", h, q, g)]
+            nc.vector.tensor_tensor(
+                out=m_g[:, h, g, q * 1024 : (q + 1) * 1024].rearrange("p (c u e) -> p c u e", u=2, e=2),
+                in0=bank[:].bitcast(BF16).rearrange("p (u c e) -> p c u e", u=2, e=2),
+                in1=m_fac[:, g, :].rearrange("p (u e) -> p u e", e=2).unsqueeze(1).to_broadcast([128, 256, 2, 2]),
+                op=ALU.mult,
+            )
+
+        def order_at(g):
+            nc.vector.tensor_copy(
+                out=at_c[:, g, :].rearrange("p (k t c) -> p k c t", t=4, c=128),
+                in_=at_raw[:, g, :].rearrange("p (k c t) -> p k c t", t=4, c=128),
+            )
+
+        def order_at_scales(engine="v"):
+            copy = nc.vector.tensor_copy if engine == "v" else nc.gpsimd.tensor_copy
+            copy(
+                out=at_s[:].rearrange("p (k t c) -> p k c t", t=4, c=128),
+                in_=at_sraw[:].rearrange("p (k c t) -> p k c t", t=4, c=128),
+            )
+
+        def memory(h, k, t):
+            bank = psum.tile([128, 512], F32, name="bank")
+            lo = k * 512 + t * 128
+            for g in range(GM):
+                nc.tensor.matmul_mx(
+                    out=bank[:],
+                    lhsT=at_c[:, g, lo : lo + 128].bitcast(FP8X4),
+                    lhsT_scale=at_s[4 * g : 128, lo : lo + 128],
+                    rhs=m_c[:, h, g, :].bitcast(FP8X4),
+                    rhs_scale=m_s[:, h, g, :],
+                    start=(g == 0),
+                    stop=(g == GM - 1),
+                )
+            banks[("n", h, k, t)] = bank
+
+        def take_memory(h, k, t):
+            bank = banks[("n", h, k, t)]
+            nc.vector.scalar_tensor_tensor(
+                out=n_p[:, h, k, t, :],
+                in0=u_bc[:, h, :],
+                scalar=b_col[:, k, t : t + 1],
+                in1=bank[:],
+                op0=ALU.mult,
+                op1=ALU.add,
+            )
+
+        def interleave(h, k, engine):
+            dst = n_g[:, h, k, :].rearrange("p (c t) -> p c t", t=4)
+            src = n_p[:, h, k, :, :].rearrange("p t c -> p c t")
+            if engine == "v":
+                nc.vector.tensor_copy(out=dst, in_=src)
+            else:
+                nc.scalar.copy(out=dst, in_=src)
+
+        def finish(h, r, c):
+            bank = psum.tile([128, 512], F32, name="bank")
+            rows = slice(r * 128, (r + 1) * 128)
+            cols = slice(c * 512, (c + 1) * 512)
+            for g in range(GZ):
+                nc.tensor.matmul_mx(
+                    out=bank[:],
+                    lhsT=z_c[:, h, g, rows].bitcast(FP8X4),
+                    lhsT_scale=z_s[:, h, g, rows],
+                    rhs=wz_c[:, g, cols].bitcast(FP8X4),
+                    rhs_scale=wz_s[4 * g : 128, cols],
+                    start=(g == 0),
+                    stop=False,
+                )
+            for g in range(GM):
+                nc.tensor.matmul_mx(
+                    out=bank[:],
+                    lhsT=n_c[:, h, g, rows].bitcast(FP8X4),
+                    lhsT_scale=n_s[:, h, g, rows],
+                    rhs=wm_c[:, g, cols].bitcast(FP8X4),
+                    rhs_scale=wm_s[4 * g : 128, cols],
+                    start=False,
+                    stop=(g == GM - 1),
+                )
+            res = results.tile([128, 512], F32, name="res")
+            nc.scalar.activation(out=res[:], in_=bank[:], func=ACT.Tanh)
+            nc.sync.dma_start(out=out_rows[h][:, r, cols], in_=res[:])
+
+        make_identity(nc, ident[:])
+        nc.vector.memset(warm[:], 0.0)
+        nc.vector.memset(at_sraw[:].bitcast(I32), 0)
+        nc.vector.memset(wz_s[:].bitcast(I32), 0)
+        nc.vector.memset(wm_s[:].bitcast(I32), 0)
+        nc.scalar.dma_start(out=ez_col[:], in_=ez.rearrange("(g p t) -> p g t", p=128, t=4))
+        nc.scalar.dma_start(out=m_fac[:], in_=m_scale.rearrange("o (g p t) -> p (o g) t", p=128, t=4))
+        nc.scalar.dma_start(out=b_col[:], in_=bvec.rearrange("(g p t) -> p g t", p=128, t=4))
+        nc.scalar.activation(out=warm[:], in_=warm[:], func=ACT.Tanh)
+
+        load_z(0, 0)
+        load_z(0, 1)
+        load_m(0)
+        load_z(0, 2)
+        load_z(0, 3)
+        load_z(1, 0)
+        load_z(1, 1)
+        load_words(at_raw, at_words, 0)
+        load_words(at_raw, at_words, 1)
+        load_z(1, 2)
+        load_z(1, 3)
+        load_scales(at_sraw, at_scales, GM)
+        load_m(1)
+        for g in range(GZ):
+            load_words(wz_c, wz_words, g)
+        load_scales(wz_s, wz_scales, GZ)
+        for g in range(GM):
+            load_words(wm_c, wm_words, g)
+        load_scales(wm_s, wm_scales, GM)
+
+        for g in range(GZ):
+            turn_z(0, 0, g, direct=True)
+            take_z(0, 0, g)
+        cast_m(0, 0, "v")
+        pre_z(0, 2)
+        pre_z(0, 3)
+        cast_m(0, 1)
+        write_scalar(0, 0)
+        for g in range(GM):
+            turn_m(0, 0, g)
+        for g in range(GZ):
+            turn_z(0, 1, g)
+            take_z(0, 1, g)
+        for g in range(GM):
+            take_m(0, 0, g)
+        pre_z(1, 0, "s")
+        pre_z(1, 1, "s")
+        for g in range(GM):
+            turn_m(0, 1, g)
+        take_scalar(0, 0)
+        write_scalar(0, 1)
+        for g in range(GM):
+            take_m(0, 1, g)
+        order_at(0)
+        for g in range(GZ):
+            turn_z(1, 0, g)
+            take_z(1, 0, g)
+        order_at(1)
+        take_scalar(0, 1)
+        write_scalar(1, 0)
+        pre_z(1, 2)
+        pre_z(1, 3)
+        for g in range(GM):
+            quant(m_g, m_c, m_s, 0, g)
+        order_at_scales("g")
+        for g in range(GZ):
+            turn_z(1, 1, g)
+            take_z(1, 1, g)
+        cast_m(1, 0)
+        take_scalar(1, 0)
+        for k in range(GM):
+            for t in range(4):
+                memory(0, k, t)
+                take_memory(0, k, t)
+        write_scalar(1, 1)
+        cast_m(1, 1)
+        take_scalar(1, 1)
+        for q in range(2):
+            for g in range(GM):
+                turn_m(1, q, g)
+        for k in range(GM):
+            interleave(0, k, "s" if k == 0 else "v")
+        for g in range(GZ):
+            quant(z_g, z_c, z_s, 0, g)
+        for g in range(GM):
+            quant(n_g, n_c, n_s, 0, g)
+        for q in range(2):
+            for g in range(GM):
+                take_m(1, q, g)
+        for g in range(GM):
+            quant(m_g, m_c, m_s, 1, g)
+        for r in range(2):
+            for c in range(2):
+                finish(0, r, c)
+        for k in range(GM):
+            for t in range(4):
+                memory(1, k, t)
+                take_memory(1, k, t)
+            interleave(1, k, "v")
+        for g in range(GZ):
+            quant(z_g, z_c, z_s, 1, g)
+        for g in range(GM):
+            quant(n_g, n_c, n_s, 1, g)
+        for r in range(2, 4):
+            for c in range(2):
+                finish(0, r, c)
+        for r in range(4):
+            for c in range(2):
+                finish(1, r, c)

@@ -26,7 +26,8 @@ def tile_legendrememoryunitstep_w8_kernel(
     with ExitStack() as ctx:
         keep = ctx.enter_context(tc.tile_pool(name="keep", bufs=1))
         stage = ctx.enter_context(tc.tile_pool(name="stage", bufs=8))
-        work = ctx.enter_context(tc.tile_pool(name="work", bufs=3))
+        zwords = ctx.enter_context(tc.tile_pool(name="zwords", bufs=6))
+        work = ctx.enter_context(tc.tile_pool(name="work", bufs=2))
         results = ctx.enter_context(tc.tile_pool(name="results", bufs=4))
         psum = ctx.enter_context(tc.psum_pool(name="psum", bufs=8))
         ctx.enter_context(tc.manual_schedule())
@@ -63,12 +64,20 @@ def tile_legendrememoryunitstep_w8_kernel(
         zin = {}
         zpre = {}
         m_bf = {}
+        m_pre = {}
         banks = {}
 
-        def load_z(h, r):
-            zt = stage.tile([128, K], BF16, name="zt")
-            nc.sync.dma_start(out=zt[:], in_=z_rows[h][:, r, :])
-            zin[(h, r)] = zt
+        def load_z(h, r, lo=0, hi=K):
+            if (h, r) not in zin:
+                zt = stage.tile([128, K], BF16, name="zt")
+                zin[(h, r)] = zt
+            nc.sync.dma_start(out=zin[(h, r)][:, lo:hi], in_=z_rows[h][:, r, lo:hi])
+
+        def load_small(tile, src):
+            nc.sync.dma_start(out=tile[:], in_=src)
+
+        def warm_up():
+            nc.tensor.matmul(warm_bank[:], lhsT=zeros[:, 0:128], rhs=zeros[:], start=True, stop=True)
 
         def load_m(h):
             nc.sync.dma_start(out=m_raw[:, h, :], in_=m_rows[h])
@@ -84,7 +93,7 @@ def tile_legendrememoryunitstep_w8_kernel(
                 )
 
         def pre_z(h, r, engine="v"):
-            zp = stage.tile([128, K // 2], F32, name="zp")
+            zp = zwords.tile([128, K // 2], F32, name="zp")
             copy = nc.vector.tensor_copy if engine == "v" else nc.scalar.copy
             copy(
                 out=zp[:].rearrange("p (u c) -> p u c", u=2),
@@ -141,15 +150,28 @@ def tile_legendrememoryunitstep_w8_kernel(
             copy(out=mt[:], in_=m_raw[:, h, q * 2048 : (q + 1) * 2048].bitcast(FP8))
             m_bf[(h, q)] = mt
 
+        def pre_m(h, q, engine="v"):
+            mp = work.tile([128, 1024], F32, name="mp")
+            copy = nc.vector.tensor_copy if engine == "v" else nc.scalar.copy
+            copy(
+                out=mp[:].rearrange("p (u c) -> p u c", u=2),
+                in_=m_bf[(h, q)][:].bitcast(F32).rearrange("p (c u) -> p u c", u=2),
+            )
+            m_pre[(h, q)] = mp
+
         def turn_m(h, q, g):
             bank = psum.tile([128, 512], F32, name="bank")
-            words = m_bf[(h, q)][:].bitcast(F32)
             for j in range(2):
                 for u in range(2):
-                    lo = 512 * j + 256 * g
+                    if (h, q) in m_pre:
+                        lo = 512 * u + 256 * j + 128 * g
+                        words = m_pre[(h, q)][:, lo : lo + 128]
+                    else:
+                        lo = 512 * j + 256 * g
+                        words = m_bf[(h, q)][:].bitcast(F32)[:, lo + u : lo + 256 : 2]
                     nc.tensor.transpose(
                         bank[:, u * 256 + j * 128 : u * 256 + (j + 1) * 128],
-                        words[:, lo + u : lo + 256 : 2],
+                        words,
                         ident[:],
                     )
             banks[("m", h, q, g)] = bank
@@ -210,8 +232,9 @@ def tile_legendrememoryunitstep_w8_kernel(
             else:
                 nc.scalar.copy(out=dst, in_=src)
 
-        def finish(h, r, c):
+        def finish_z(h, r, c):
             bank = psum.tile([128, 512], F32, name="bank")
+            banks[("f", h, r, c)] = bank
             rows = slice(r * 128, (r + 1) * 128)
             cols = slice(c * 512, (c + 1) * 512)
             for g in range(GZ):
@@ -224,6 +247,11 @@ def tile_legendrememoryunitstep_w8_kernel(
                     start=(g == 0),
                     stop=False,
                 )
+
+        def finish_n(h, r, c):
+            bank = banks[("f", h, r, c)]
+            rows = slice(r * 128, (r + 1) * 128)
+            cols = slice(c * 512, (c + 1) * 512)
             for g in range(GM):
                 nc.tensor.matmul_mx(
                     out=bank[:],
@@ -234,116 +262,230 @@ def tile_legendrememoryunitstep_w8_kernel(
                     start=False,
                     stop=(g == GM - 1),
                 )
+
+        def squash(h, r, c):
             res = results.tile([128, 512], F32, name="res")
-            nc.scalar.activation(out=res[:], in_=bank[:], func=ACT.Tanh)
-            nc.sync.dma_start(out=out_rows[h][:, r, cols], in_=res[:])
+            nc.scalar.activation(out=res[:], in_=banks[("f", h, r, c)][:], func=ACT.Tanh)
+            banks[("r", h, r, c)] = res
+
+        def store(h, r, c):
+            nc.sync.dma_start(out=out_rows[h][:, r, c * 512 : (c + 1) * 512], in_=banks[("r", h, r, c)][:])
 
         make_identity(nc, ident[:])
         nc.vector.memset(warm[:], 0.0)
+        zeros = keep.tile([128, 512], BF16, name="zeros")
+        nc.vector.memset(zeros[:], 0.0)
+        warm_bank = psum.tile([128, 512], F32, name="bank")
         nc.vector.memset(at_sraw[:].bitcast(I32), 0)
         nc.vector.memset(wz_s[:].bitcast(I32), 0)
         nc.vector.memset(wm_s[:].bitcast(I32), 0)
-        nc.scalar.dma_start(out=ez_col[:], in_=ez.rearrange("(g p t) -> p g t", p=128, t=4))
-        nc.scalar.dma_start(out=m_fac[:], in_=m_scale.rearrange("o (g p t) -> p (o g) t", p=128, t=4))
-        nc.scalar.dma_start(out=b_col[:], in_=bvec.rearrange("(g p t) -> p g t", p=128, t=4))
         nc.scalar.activation(out=warm[:], in_=warm[:], func=ACT.Tanh)
-
-        load_z(0, 0)
-        load_z(0, 1)
+        warm_up()
+        warm_up()
         load_m(0)
-        load_z(0, 2)
-        load_z(0, 3)
-        load_z(1, 0)
-        load_z(1, 1)
-        load_words(at_raw, at_words, 0)
-        load_words(at_raw, at_words, 1)
-        load_z(1, 2)
+        warm_up()
+        cast_m(0, 1, "s")
+        warm_up()
         load_z(1, 3)
-        load_scales(at_sraw, at_scales, GM)
-        load_m(1)
-        for g in range(GZ):
-            load_words(wz_c, wz_words, g)
-        load_scales(wz_s, wz_scales, GZ)
-        for g in range(GM):
-            load_words(wm_c, wm_words, g)
-        load_scales(wm_s, wm_scales, GM)
-
-        for g in range(GZ):
-            turn_z(0, 0, g, direct=True)
-            take_z(0, 0, g)
+        pre_z(1, 3, "s")
+        load_z(0, 1, 0, 512)
         cast_m(0, 0, "v")
-        pre_z(0, 2)
-        pre_z(0, 3)
-        cast_m(0, 1)
-        write_scalar(0, 0)
-        for g in range(GM):
-            turn_m(0, 0, g)
-        for g in range(GZ):
-            turn_z(0, 1, g)
-            take_z(0, 1, g)
-        for g in range(GM):
-            take_m(0, 0, g)
-        pre_z(1, 0, "s")
-        pre_z(1, 1, "s")
-        for g in range(GM):
-            turn_m(0, 1, g)
-        take_scalar(0, 0)
-        write_scalar(0, 1)
-        for g in range(GM):
-            take_m(0, 1, g)
-        order_at(0)
-        for g in range(GZ):
-            turn_z(1, 0, g)
-            take_z(1, 0, g)
+        pre_m(0, 0, "v")
+        turn_m(0, 0, 0)
+        turn_m(0, 0, 1)
+        pre_m(0, 1, "s")
+        load_z(1, 2)
+        pre_z(1, 2, "v")
+        turn_z(1, 1, 1)
+        take_z(1, 1, 1, "s")
+        turn_z(1, 1, 2)
+        take_z(1, 1, 2, "s")
+        warm_up()
+        load_z(0, 0, 512, K)
+        load_small(m_fac, m_scale.rearrange("o (g p t) -> p (o g) t", p=128, t=4))
+        take_m(0, 0, 0)
+        take_m(0, 0, 1)
+        turn_m(0, 1, 1)
+        load_small(b_col, bvec.rearrange("(g p t) -> p g t", p=128, t=4))
+        load_z(0, 2)
+        pre_z(0, 2, "v")
+        take_m(0, 1, 1)
+        turn_m(0, 1, 0)
+        take_m(0, 1, 0)
+        quant(m_g, m_c, m_s, 0, 0)
+        turn_z(1, 1, 0)
+        load_z(0, 3)
+        pre_z(0, 3, "s")
+        turn_z(0, 1, 1)
+        take_z(0, 1, 1, "s")
+        turn_z(0, 1, 2)
+        turn_z(0, 1, 0)
+        take_z(0, 1, 0, "s")
+        take_z(0, 1, 2, "s")
+        take_z(1, 1, 0, "s")
+        quant(m_g, m_c, m_s, 0, 1)
+        load_z(0, 1, 512, K)
+        turn_z(0, 0, 2, direct=True)
+        take_z(0, 0, 2, "s")
+        turn_z(0, 0, 1, direct=True)
+        load_words(at_raw, at_words, 1)
         order_at(1)
-        take_scalar(0, 1)
-        write_scalar(1, 0)
-        pre_z(1, 2)
-        pre_z(1, 3)
-        for g in range(GM):
-            quant(m_g, m_c, m_s, 0, g)
-        order_at_scales("g")
-        for g in range(GZ):
-            turn_z(1, 1, g)
-            take_z(1, 1, g)
-        cast_m(1, 0)
-        take_scalar(1, 0)
-        for k in range(GM):
-            for t in range(4):
-                memory(0, k, t)
-                take_memory(0, k, t)
+        load_z(0, 0, 0, 512)
+        turn_z(0, 0, 0, direct=True)
+        take_z(0, 0, 0, "v")
+        take_z(0, 0, 1, "s")
+        quant(z_g, z_c, z_s, 0, 1)
+        quant(z_g, z_c, z_s, 0, 2)
+        load_m(1)
+        cast_m(1, 1, "s")
+        load_small(ez_col, ez.rearrange("(g p t) -> p g t", p=128, t=4))
+        write_scalar(0, 1)
         write_scalar(1, 1)
-        cast_m(1, 1)
-        take_scalar(1, 1)
-        for q in range(2):
-            for g in range(GM):
-                turn_m(1, q, g)
-        for k in range(GM):
-            interleave(0, k, "s" if k == 0 else "v")
-        for g in range(GZ):
-            quant(z_g, z_c, z_s, 0, g)
-        for g in range(GM):
-            quant(n_g, n_c, n_s, 0, g)
-        for q in range(2):
-            for g in range(GM):
-                take_m(1, q, g)
-        for g in range(GM):
-            quant(m_g, m_c, m_s, 1, g)
-        for r in range(2):
-            for c in range(2):
-                finish(0, r, c)
-        for k in range(GM):
-            for t in range(4):
-                memory(1, k, t)
-                take_memory(1, k, t)
-            interleave(1, k, "v")
-        for g in range(GZ):
-            quant(z_g, z_c, z_s, 1, g)
-        for g in range(GM):
-            quant(n_g, n_c, n_s, 1, g)
-        for r in range(2, 4):
-            for c in range(2):
-                finish(0, r, c)
-        for r in range(4):
-            for c in range(2):
-                finish(1, r, c)
+        write_scalar(0, 0)
+        take_scalar(1, 1, "s")
+        take_scalar(0, 1, "s")
+        load_words(at_raw, at_words, 0)
+        order_at(0)
+        load_scales(at_sraw, at_scales, GM)
+        order_at_scales("v")
+        memory(0, 0, 1)
+        memory(0, 1, 0)
+        memory(0, 0, 0)
+        memory(0, 1, 3)
+        memory(0, 1, 1)
+        quant(z_g, z_c, z_s, 0, 0)
+        cast_m(1, 0, "s")
+        pre_m(1, 0, "s")
+        pre_m(1, 1, "v")
+        load_z(1, 1)
+        pre_z(1, 1, "s")
+        load_scales(wz_s, wz_scales, GZ)
+        take_scalar(0, 0, "v")
+        take_memory(0, 0, 0)
+        take_memory(0, 1, 0)
+        take_memory(0, 1, 3)
+        take_memory(0, 0, 1)
+        take_memory(0, 1, 1)
+        memory(0, 0, 3)
+        take_memory(0, 0, 3)
+        load_words(wz_c, wz_words, 1)
+        memory(0, 1, 2)
+        take_memory(0, 1, 2)
+        memory(0, 0, 2)
+        take_memory(0, 0, 2)
+        load_z(1, 0)
+        pre_z(1, 0, "s")
+        turn_z(1, 0, 2)
+        take_z(1, 0, 2, "s")
+        turn_z(1, 0, 1)
+        take_z(1, 0, 1, "s")
+        interleave(0, 0, "v")
+        quant(n_g, n_c, n_s, 0, 0)
+        load_scales(wm_s, wm_scales, GM)
+        quant(z_g, z_c, z_s, 1, 2)
+        turn_z(1, 0, 0)
+        take_z(1, 0, 0, "s")
+        load_words(wz_c, wz_words, 2)
+        load_words(wm_c, wm_words, 1)
+        interleave(0, 1, "s")
+        quant(n_g, n_c, n_s, 0, 1)
+        turn_m(1, 0, 1)
+        take_m(1, 0, 1)
+        load_words(wm_c, wm_words, 0)
+        turn_m(1, 0, 0)
+        take_m(1, 0, 0)
+        turn_m(1, 1, 0)
+        take_m(1, 1, 0)
+        quant(m_g, m_c, m_s, 1, 0)
+        turn_m(1, 1, 1)
+        write_scalar(1, 0)
+        take_scalar(1, 0, "s")
+        take_m(1, 1, 1)
+        load_words(wz_c, wz_words, 0)
+        finish_z(0, 1, 0)
+        finish_z(0, 1, 1)
+        finish_n(0, 1, 1)
+        squash(0, 1, 1)
+        store(0, 1, 1)
+        finish_z(0, 0, 1)
+        finish_n(0, 0, 1)
+        finish_n(0, 1, 0)
+        squash(0, 1, 0)
+        store(0, 1, 0)
+        squash(0, 0, 1)
+        store(0, 0, 1)
+        finish_z(0, 3, 1)
+        finish_n(0, 3, 1)
+        squash(0, 3, 1)
+        store(0, 3, 1)
+        finish_z(0, 3, 0)
+        finish_n(0, 3, 0)
+        squash(0, 3, 0)
+        store(0, 3, 0)
+        finish_z(0, 2, 0)
+        finish_n(0, 2, 0)
+        squash(0, 2, 0)
+        store(0, 2, 0)
+        quant(z_g, z_c, z_s, 1, 1)
+        quant(m_g, m_c, m_s, 1, 1)
+        memory(1, 1, 0)
+        memory(1, 0, 0)
+        take_memory(1, 1, 0)
+        memory(1, 1, 2)
+        take_memory(1, 0, 0)
+        take_memory(1, 1, 2)
+        memory(1, 1, 3)
+        take_memory(1, 1, 3)
+        memory(1, 1, 1)
+        take_memory(1, 1, 1)
+        interleave(1, 1, "s")
+        memory(1, 0, 3)
+        take_memory(1, 0, 3)
+        memory(1, 0, 1)
+        take_memory(1, 0, 1)
+        memory(1, 0, 2)
+        take_memory(1, 0, 2)
+        finish_z(0, 2, 1)
+        finish_n(0, 2, 1)
+        squash(0, 2, 1)
+        store(0, 2, 1)
+        finish_z(0, 0, 0)
+        finish_n(0, 0, 0)
+        squash(0, 0, 0)
+        store(0, 0, 0)
+        quant(z_g, z_c, z_s, 1, 0)
+        finish_z(1, 3, 1)
+        finish_z(1, 2, 0)
+        finish_z(1, 2, 1)
+        finish_z(1, 3, 0)
+        finish_z(1, 0, 1)
+        finish_z(1, 0, 0)
+        finish_z(1, 1, 0)
+        interleave(1, 0, "v")
+        quant(n_g, n_c, n_s, 1, 0)
+        quant(n_g, n_c, n_s, 1, 1)
+        finish_n(1, 2, 0)
+        finish_n(1, 1, 0)
+        squash(1, 1, 0)
+        store(1, 1, 0)
+        squash(1, 2, 0)
+        store(1, 2, 0)
+        finish_n(1, 3, 0)
+        finish_n(1, 2, 1)
+        squash(1, 3, 0)
+        store(1, 3, 0)
+        finish_n(1, 0, 1)
+        squash(1, 0, 1)
+        store(1, 0, 1)
+        squash(1, 2, 1)
+        store(1, 2, 1)
+        finish_n(1, 3, 1)
+        squash(1, 3, 1)
+        store(1, 3, 1)
+        finish_n(1, 0, 0)
+        squash(1, 0, 0)
+        store(1, 0, 0)
+        finish_z(1, 1, 1)
+        finish_n(1, 1, 1)
+        squash(1, 1, 1)
+        store(1, 1, 1)

@@ -26,9 +26,10 @@ def tile_legendrememoryunitstep_w8_kernel(
     with ExitStack() as ctx:
         keep = ctx.enter_context(tc.tile_pool(name="keep", bufs=1))
         stage = ctx.enter_context(tc.tile_pool(name="stage", bufs=8))
-        zwords = ctx.enter_context(tc.tile_pool(name="zwords", bufs=6))
-        work = ctx.enter_context(tc.tile_pool(name="work", bufs=2))
-        results = ctx.enter_context(tc.tile_pool(name="results", bufs=4))
+        zwords = ctx.enter_context(tc.tile_pool(name="zwords", bufs=4))
+        mrows = ctx.enter_context(tc.tile_pool(name="mrows", bufs=4))
+        mwords = ctx.enter_context(tc.tile_pool(name="mwords", bufs=4))
+        results = ctx.enter_context(tc.tile_pool(name="results", bufs=8))
         psum = ctx.enter_context(tc.psum_pool(name="psum", bufs=8))
         ctx.enter_context(tc.manual_schedule())
 
@@ -77,10 +78,12 @@ def tile_legendrememoryunitstep_w8_kernel(
             nc.sync.dma_start(out=tile[:], in_=src)
 
         def warm_up():
-            nc.tensor.matmul(warm_bank[:], lhsT=zeros[:, 0:128], rhs=zeros[:], start=True, stop=True)
+            bank = psum.tile([128, 512], F32, name="bank")
+            nc.tensor.matmul(bank[:], lhsT=zeros[:, 0:128], rhs=zeros[:], start=True, stop=True)
 
-        def load_m(h):
-            nc.sync.dma_start(out=m_raw[:, h, :], in_=m_rows[h])
+        def load_m(h, q):
+            cols = slice(q * 2048, (q + 1) * 2048)
+            nc.sync.dma_start(out=m_raw[:, h, cols], in_=m_rows[h][:, cols])
 
         def load_words(tile, words, g):
             nc.sync.dma_start(out=tile[:, g, :], in_=words[g].rearrange("p n t -> p (n t)").bitcast(I32))
@@ -127,48 +130,47 @@ def tile_legendrememoryunitstep_w8_kernel(
         def quant(src, codes, scales, h, g):
             nc.vector.quantize_mx(out=codes[:, h, g, :].bitcast(FP8X4), scales=scales[:, h, g, :], in_=src[:, h, g, :])
 
-        def write_scalar(h, q):
-            bank = psum.tile([128, 512], F32, name="bank")
-            for g in range(GZ):
-                for t in range(4):
-                    nc.tensor.matmul(
-                        bank[:, 0:256],
-                        lhsT=ez_col[:, g, t : t + 1].to_broadcast([128, 128]),
-                        rhs=z_g[:, h, g, q * 1024 : (q + 1) * 1024].rearrange("p (c t) -> p t c", t=4)[:, t, :],
-                        start=(g == 0 and t == 0),
-                        stop=(g == GZ - 1 and t == 3),
-                    )
-            banks[("u", h, q)] = bank
+        def write_scalar(h, q, g):
+            if g == 0:
+                bank = psum.tile([128, 512], F32, name="bank")
+                banks[("u", h, q)] = bank
+            for t in range(4):
+                nc.tensor.matmul(
+                    banks[("u", h, q)][:, 0:256],
+                    lhsT=ez_col[:, g, t : t + 1].to_broadcast([128, 128]),
+                    rhs=z_g[:, h, g, q * 1024 : (q + 1) * 1024].rearrange("p (c t) -> p t c", t=4)[:, t, :],
+                    start=(g == 0 and t == 0),
+                    stop=(g == GZ - 1 and t == 3),
+                )
 
         def take_scalar(h, q, engine="s"):
             copy = nc.vector.tensor_copy if engine == "v" else nc.scalar.copy
             copy(out=u_bc[:, h, q * 256 : (q + 1) * 256], in_=banks[("u", h, q)][:, 0:256])
 
-        def cast_m(h, q, engine="s"):
-            mt = work.tile([128, 2048], BF16, name="mt")
+        def cast_m(h, r, engine="s"):
+            mt = mrows.tile([128, 1024], BF16, name="mt")
             copy = nc.vector.tensor_copy if engine == "v" else nc.scalar.copy
-            copy(out=mt[:], in_=m_raw[:, h, q * 2048 : (q + 1) * 2048].bitcast(FP8))
-            m_bf[(h, q)] = mt
+            copy(out=mt[:], in_=m_raw[:, h, r * 1024 : (r + 1) * 1024].bitcast(FP8))
+            m_bf[(h, r)] = mt
 
-        def pre_m(h, q, engine="v"):
-            mp = work.tile([128, 1024], F32, name="mp")
+        def pre_m(h, r, engine="v"):
+            mp = mwords.tile([128, 512], F32, name="mp")
             copy = nc.vector.tensor_copy if engine == "v" else nc.scalar.copy
             copy(
                 out=mp[:].rearrange("p (u c) -> p u c", u=2),
-                in_=m_bf[(h, q)][:].bitcast(F32).rearrange("p (c u) -> p u c", u=2),
+                in_=m_bf[(h, r)][:].bitcast(F32).rearrange("p (c u) -> p u c", u=2),
             )
-            m_pre[(h, q)] = mp
+            m_pre[(h, r)] = mp
 
         def turn_m(h, q, g):
             bank = psum.tile([128, 512], F32, name="bank")
             for j in range(2):
+                r = 2 * q + j
                 for u in range(2):
-                    if (h, q) in m_pre:
-                        lo = 512 * u + 256 * j + 128 * g
-                        words = m_pre[(h, q)][:, lo : lo + 128]
+                    if (h, r) in m_pre:
+                        words = m_pre[(h, r)][:, 256 * u + 128 * g : 256 * u + 128 * (g + 1)]
                     else:
-                        lo = 512 * j + 256 * g
-                        words = m_bf[(h, q)][:].bitcast(F32)[:, lo + u : lo + 256 : 2]
+                        words = m_bf[(h, r)][:].bitcast(F32)[:, 256 * g + u : 256 * (g + 1) : 2]
                     nc.tensor.transpose(
                         bank[:, u * 256 + j * 128 : u * 256 + (j + 1) * 128],
                         words,
@@ -236,10 +238,11 @@ def tile_legendrememoryunitstep_w8_kernel(
             bank = psum.tile([128, 512], F32, name="bank")
             banks[("f", h, r, c)] = bank
             rows = slice(r * 128, (r + 1) * 128)
-            cols = slice(c * 512, (c + 1) * 512)
+            w = 256 if (h, r) == (1, 3) else 512
+            cols = slice(c * w, (c + 1) * w)
             for g in range(GZ):
                 nc.tensor.matmul_mx(
-                    out=bank[:],
+                    out=bank[:, 0:w],
                     lhsT=z_c[:, h, g, rows].bitcast(FP8X4),
                     lhsT_scale=z_s[:, h, g, rows],
                     rhs=wz_c[:, g, cols].bitcast(FP8X4),
@@ -251,10 +254,11 @@ def tile_legendrememoryunitstep_w8_kernel(
         def finish_n(h, r, c):
             bank = banks[("f", h, r, c)]
             rows = slice(r * 128, (r + 1) * 128)
-            cols = slice(c * 512, (c + 1) * 512)
+            w = 256 if (h, r) == (1, 3) else 512
+            cols = slice(c * w, (c + 1) * w)
             for g in range(GM):
                 nc.tensor.matmul_mx(
-                    out=bank[:],
+                    out=bank[:, 0:w],
                     lhsT=n_c[:, h, g, rows].bitcast(FP8X4),
                     lhsT_scale=n_s[:, h, g, rows],
                     rhs=wm_c[:, g, cols].bitcast(FP8X4),
@@ -265,227 +269,253 @@ def tile_legendrememoryunitstep_w8_kernel(
 
         def squash(h, r, c):
             res = results.tile([128, 512], F32, name="res")
-            nc.scalar.activation(out=res[:], in_=banks[("f", h, r, c)][:], func=ACT.Tanh)
+            w = 256 if (h, r) == (1, 3) else 512
+            nc.scalar.activation(out=res[:, 0:w], in_=banks[("f", h, r, c)][:, 0:w], func=ACT.Tanh)
             banks[("r", h, r, c)] = res
 
         def store(h, r, c):
-            nc.sync.dma_start(out=out_rows[h][:, r, c * 512 : (c + 1) * 512], in_=banks[("r", h, r, c)][:])
+            w = 256 if (h, r) == (1, 3) else 512
+            nc.sync.dma_start(out=out_rows[h][:, r, c * w : (c + 1) * w], in_=banks[("r", h, r, c)][:, 0:w])
 
         make_identity(nc, ident[:])
         nc.vector.memset(warm[:], 0.0)
         zeros = keep.tile([128, 512], BF16, name="zeros")
         nc.vector.memset(zeros[:], 0.0)
-        warm_bank = psum.tile([128, 512], F32, name="bank")
         nc.vector.memset(at_sraw[:].bitcast(I32), 0)
         nc.vector.memset(wz_s[:].bitcast(I32), 0)
         nc.vector.memset(wm_s[:].bitcast(I32), 0)
         nc.scalar.activation(out=warm[:], in_=warm[:], func=ACT.Tanh)
+        load_m(0, 1)
+        cast_m(0, 3, "s")
         warm_up()
         warm_up()
-        load_m(0)
         warm_up()
-        cast_m(0, 1, "s")
+        load_small(ez_col, ez.rearrange("(g p t) -> p g t", p=128, t=4))
         warm_up()
-        load_z(1, 3)
-        pre_z(1, 3, "s")
-        load_z(0, 1, 0, 512)
+        warm_up()
+        cast_m(0, 2, "v")
+        load_m(0, 0)
         cast_m(0, 0, "v")
-        pre_m(0, 0, "v")
-        turn_m(0, 0, 0)
-        turn_m(0, 0, 1)
-        pre_m(0, 1, "s")
-        load_z(1, 2)
-        pre_z(1, 2, "v")
-        turn_z(1, 1, 1)
-        take_z(1, 1, 1, "s")
-        turn_z(1, 1, 2)
-        take_z(1, 1, 2, "s")
+        cast_m(0, 1, "v")
         warm_up()
-        load_z(0, 0, 512, K)
         load_small(m_fac, m_scale.rearrange("o (g p t) -> p (o g) t", p=128, t=4))
-        take_m(0, 0, 0)
-        take_m(0, 0, 1)
-        turn_m(0, 1, 1)
-        load_small(b_col, bvec.rearrange("(g p t) -> p g t", p=128, t=4))
-        load_z(0, 2)
-        pre_z(0, 2, "v")
-        take_m(0, 1, 1)
         turn_m(0, 1, 0)
         take_m(0, 1, 0)
-        quant(m_g, m_c, m_s, 0, 0)
-        turn_z(1, 1, 0)
-        load_z(0, 3)
-        pre_z(0, 3, "s")
-        turn_z(0, 1, 1)
-        take_z(0, 1, 1, "s")
-        turn_z(0, 1, 2)
-        turn_z(0, 1, 0)
-        take_z(0, 1, 0, "s")
-        take_z(0, 1, 2, "s")
-        take_z(1, 1, 0, "s")
-        quant(m_g, m_c, m_s, 0, 1)
-        load_z(0, 1, 512, K)
-        turn_z(0, 0, 2, direct=True)
-        take_z(0, 0, 2, "s")
-        turn_z(0, 0, 1, direct=True)
-        load_words(at_raw, at_words, 1)
-        order_at(1)
-        load_z(0, 0, 0, 512)
-        turn_z(0, 0, 0, direct=True)
-        take_z(0, 0, 0, "v")
-        take_z(0, 0, 1, "s")
-        quant(z_g, z_c, z_s, 0, 1)
-        quant(z_g, z_c, z_s, 0, 2)
-        load_m(1)
+        warm_up()
+        load_m(1, 0)
+        cast_m(1, 0, "s")
         cast_m(1, 1, "s")
-        load_small(ez_col, ez.rearrange("(g p t) -> p g t", p=128, t=4))
-        write_scalar(0, 1)
-        write_scalar(1, 1)
-        write_scalar(0, 0)
-        take_scalar(1, 1, "s")
-        take_scalar(0, 1, "s")
-        load_words(at_raw, at_words, 0)
-        order_at(0)
+        pre_m(1, 0, "s")
+        pre_m(1, 1, "s")
+        load_z(0, 3)
+        warm_up()
+        turn_m(0, 0, 1)
+        load_z(0, 0, 0, 512)
+        take_m(0, 0, 1)
+        turn_m(0, 0, 0)
+        load_z(0, 1, 0, 512)
+        turn_z(0, 0, 0, direct=True)
+        take_z(0, 0, 0, "s")
+        warm_up()
+        load_small(b_col, bvec.rearrange("(g p t) -> p g t", p=128, t=4))
+        warm_up()
+        take_m(0, 0, 0)
+        quant(m_g, m_c, m_s, 0, 0)
+        load_z(0, 2)
+        turn_z(0, 1, 0, direct=True)
+        take_z(0, 1, 0, "s")
+        turn_z(0, 1, 2, direct=True)
+        turn_z(0, 1, 1, direct=True)
+        write_scalar(0, 1, 0)
+        take_z(0, 1, 2, "s")
+        take_z(0, 1, 1, "s")
+        quant(z_g, z_c, z_s, 0, 0)
+        load_z(0, 1, 512, K)
         load_scales(at_sraw, at_scales, GM)
         order_at_scales("v")
-        memory(0, 0, 1)
-        memory(0, 1, 0)
-        memory(0, 0, 0)
-        memory(0, 1, 3)
-        memory(0, 1, 1)
-        quant(z_g, z_c, z_s, 0, 0)
-        cast_m(1, 0, "s")
-        pre_m(1, 0, "s")
-        pre_m(1, 1, "v")
+        load_z(1, 0)
+        pre_z(1, 0, "s")
+        turn_m(1, 0, 0)
+        take_m(1, 0, 0)
+        load_z(0, 0, 512, K)
+        turn_z(0, 0, 1, direct=True)
+        take_z(0, 0, 1, "s")
+        load_words(at_raw, at_words, 0)
+        order_at(0)
+        turn_z(0, 0, 2, direct=True)
+        take_z(0, 0, 2, "s")
+        quant(z_g, z_c, z_s, 0, 2)
+        write_scalar(0, 1, 1)
+        write_scalar(0, 1, 2)
+        take_scalar(0, 1, "s")
+        write_scalar(0, 0, 0)
+        write_scalar(0, 0, 1)
+        turn_m(0, 1, 1)
         load_z(1, 1)
         pre_z(1, 1, "s")
-        load_scales(wz_s, wz_scales, GZ)
-        take_scalar(0, 0, "v")
-        take_memory(0, 0, 0)
-        take_memory(0, 1, 0)
-        take_memory(0, 1, 3)
-        take_memory(0, 0, 1)
-        take_memory(0, 1, 1)
+        turn_z(1, 0, 0)
+        take_z(1, 0, 0, "s")
+        turn_z(1, 0, 1)
+        take_z(1, 0, 1, "s")
+        turn_z(1, 0, 2)
+        take_z(1, 0, 2, "s")
+        write_scalar(0, 0, 2)
+        take_scalar(0, 0, "s")
+        load_scales(wm_s, wm_scales, GM)
+        quant(z_g, z_c, z_s, 0, 1)
+        load_z(1, 3)
+        pre_z(1, 3, "s")
+        write_scalar(1, 0, 0)
+        write_scalar(1, 0, 1)
+        write_scalar(1, 0, 2)
+        take_scalar(1, 0, "s")
+        take_m(0, 1, 1)
+        quant(m_g, m_c, m_s, 0, 1)
+        load_words(wm_c, wm_words, 0)
+        load_words(at_raw, at_words, 1)
+        order_at(1)
         memory(0, 0, 3)
         take_memory(0, 0, 3)
-        load_words(wz_c, wz_words, 1)
+        memory(0, 0, 1)
+        take_memory(0, 0, 1)
+        memory(0, 1, 1)
+        take_memory(0, 1, 1)
+        memory(0, 0, 0)
+        take_memory(0, 0, 0)
+        memory(0, 1, 0)
+        take_memory(0, 1, 0)
         memory(0, 1, 2)
         take_memory(0, 1, 2)
         memory(0, 0, 2)
         take_memory(0, 0, 2)
-        load_z(1, 0)
-        pre_z(1, 0, "s")
-        turn_z(1, 0, 2)
-        take_z(1, 0, 2, "s")
-        turn_z(1, 0, 1)
-        take_z(1, 0, 1, "s")
         interleave(0, 0, "v")
+        memory(0, 1, 3)
+        take_memory(0, 1, 3)
         quant(n_g, n_c, n_s, 0, 0)
-        load_scales(wm_s, wm_scales, GM)
-        quant(z_g, z_c, z_s, 1, 2)
-        turn_z(1, 0, 0)
-        take_z(1, 0, 0, "s")
-        load_words(wz_c, wz_words, 2)
-        load_words(wm_c, wm_words, 1)
-        interleave(0, 1, "s")
+        interleave(0, 1, "v")
         quant(n_g, n_c, n_s, 0, 1)
+        load_m(1, 1)
+        cast_m(1, 2, "s")
+        pre_m(1, 2, "s")
+        cast_m(1, 3, "s")
+        load_words(wz_c, wz_words, 1)
+        load_z(1, 2)
+        pre_z(1, 2, "s")
+        turn_z(1, 1, 0)
+        take_z(1, 1, 0, "s")
+        turn_z(1, 1, 1)
+        turn_z(1, 1, 2)
+        load_words(wz_c, wz_words, 0)
         turn_m(1, 0, 1)
         take_m(1, 0, 1)
-        load_words(wm_c, wm_words, 0)
-        turn_m(1, 0, 0)
-        take_m(1, 0, 0)
+        load_scales(wz_s, wz_scales, GZ)
+        write_scalar(1, 1, 0)
+        pre_m(1, 3, "s")
         turn_m(1, 1, 0)
         take_m(1, 1, 0)
-        quant(m_g, m_c, m_s, 1, 0)
         turn_m(1, 1, 1)
-        write_scalar(1, 0)
-        take_scalar(1, 0, "s")
         take_m(1, 1, 1)
-        load_words(wz_c, wz_words, 0)
-        finish_z(0, 1, 0)
-        finish_z(0, 1, 1)
-        finish_n(0, 1, 1)
-        squash(0, 1, 1)
-        store(0, 1, 1)
-        finish_z(0, 0, 1)
-        finish_n(0, 0, 1)
-        finish_n(0, 1, 0)
-        squash(0, 1, 0)
-        store(0, 1, 0)
-        squash(0, 0, 1)
-        store(0, 0, 1)
-        finish_z(0, 3, 1)
-        finish_n(0, 3, 1)
-        squash(0, 3, 1)
-        store(0, 3, 1)
-        finish_z(0, 3, 0)
-        finish_n(0, 3, 0)
-        squash(0, 3, 0)
-        store(0, 3, 0)
-        finish_z(0, 2, 0)
-        finish_n(0, 2, 0)
-        squash(0, 2, 0)
-        store(0, 2, 0)
-        quant(z_g, z_c, z_s, 1, 1)
         quant(m_g, m_c, m_s, 1, 1)
-        memory(1, 1, 0)
-        memory(1, 0, 0)
-        take_memory(1, 1, 0)
-        memory(1, 1, 2)
-        take_memory(1, 0, 0)
-        take_memory(1, 1, 2)
-        memory(1, 1, 3)
-        take_memory(1, 1, 3)
-        memory(1, 1, 1)
-        take_memory(1, 1, 1)
-        interleave(1, 1, "s")
-        memory(1, 0, 3)
-        take_memory(1, 0, 3)
-        memory(1, 0, 1)
-        take_memory(1, 0, 1)
-        memory(1, 0, 2)
-        take_memory(1, 0, 2)
-        finish_z(0, 2, 1)
-        finish_n(0, 2, 1)
-        squash(0, 2, 1)
-        store(0, 2, 1)
+        load_words(wm_c, wm_words, 1)
+        take_z(1, 1, 1, "s")
+        quant(z_g, z_c, z_s, 1, 1)
+        write_scalar(1, 1, 1)
+        take_z(1, 1, 2, "s")
+        write_scalar(1, 1, 2)
+        quant(z_g, z_c, z_s, 1, 2)
+        take_scalar(1, 1, "s")
+        load_words(wz_c, wz_words, 2)
+        finish_z(0, 3, 0)
+        finish_z(0, 1, 0)
         finish_z(0, 0, 0)
         finish_n(0, 0, 0)
         squash(0, 0, 0)
         store(0, 0, 0)
+        finish_z(0, 2, 1)
+        finish_n(0, 2, 1)
+        finish_z(0, 0, 1)
+        squash(0, 2, 1)
+        store(0, 2, 1)
+        finish_n(0, 1, 0)
+        squash(0, 1, 0)
+        store(0, 1, 0)
+        finish_n(0, 0, 1)
+        finish_n(0, 3, 0)
+        squash(0, 3, 0)
+        store(0, 3, 0)
+        squash(0, 0, 1)
+        store(0, 0, 1)
+        quant(m_g, m_c, m_s, 1, 0)
+        memory(1, 1, 3)
+        take_memory(1, 1, 3)
+        memory(1, 1, 0)
+        take_memory(1, 1, 0)
+        memory(1, 1, 2)
+        take_memory(1, 1, 2)
+        memory(1, 0, 3)
+        take_memory(1, 0, 3)
+        memory(1, 0, 2)
+        take_memory(1, 0, 2)
+        memory(1, 1, 1)
+        take_memory(1, 1, 1)
+        memory(1, 0, 1)
+        take_memory(1, 0, 1)
+        memory(1, 0, 0)
+        take_memory(1, 0, 0)
+        interleave(1, 0, "v")
+        interleave(1, 1, "s")
+        quant(n_g, n_c, n_s, 1, 1)
+        quant(n_g, n_c, n_s, 1, 0)
+        finish_z(0, 3, 1)
+        finish_n(0, 3, 1)
+        squash(0, 3, 1)
+        store(0, 3, 1)
+        finish_z(0, 2, 0)
+        finish_n(0, 2, 0)
+        squash(0, 2, 0)
+        store(0, 2, 0)
+        finish_z(0, 1, 1)
+        finish_n(0, 1, 1)
+        squash(0, 1, 1)
+        store(0, 1, 1)
         quant(z_g, z_c, z_s, 1, 0)
-        finish_z(1, 3, 1)
-        finish_z(1, 2, 0)
+        finish_z(1, 0, 0)
+        finish_n(1, 0, 0)
         finish_z(1, 2, 1)
         finish_z(1, 3, 0)
-        finish_z(1, 0, 1)
-        finish_z(1, 0, 0)
-        finish_z(1, 1, 0)
-        interleave(1, 0, "v")
-        quant(n_g, n_c, n_s, 1, 0)
-        quant(n_g, n_c, n_s, 1, 1)
-        finish_n(1, 2, 0)
-        finish_n(1, 1, 0)
-        squash(1, 1, 0)
-        store(1, 1, 0)
-        squash(1, 2, 0)
-        store(1, 2, 0)
         finish_n(1, 3, 0)
-        finish_n(1, 2, 1)
         squash(1, 3, 0)
         store(1, 3, 0)
+        finish_z(1, 2, 0)
+        finish_z(1, 0, 1)
         finish_n(1, 0, 1)
         squash(1, 0, 1)
         store(1, 0, 1)
-        squash(1, 2, 1)
-        store(1, 2, 1)
-        finish_n(1, 3, 1)
-        squash(1, 3, 1)
-        store(1, 3, 1)
-        finish_n(1, 0, 0)
         squash(1, 0, 0)
         store(1, 0, 0)
+        finish_n(1, 2, 0)
+        squash(1, 2, 0)
+        finish_z(1, 1, 0)
+        finish_n(1, 1, 0)
+        squash(1, 1, 0)
+        store(1, 1, 0)
+        store(1, 2, 0)
         finish_z(1, 1, 1)
         finish_n(1, 1, 1)
         squash(1, 1, 1)
         store(1, 1, 1)
+        finish_n(1, 2, 1)
+        squash(1, 2, 1)
+        store(1, 2, 1)
+        finish_z(1, 3, 3)
+        finish_n(1, 3, 3)
+        squash(1, 3, 3)
+        store(1, 3, 3)
+        finish_z(1, 3, 2)
+        finish_n(1, 3, 2)
+        squash(1, 3, 2)
+        store(1, 3, 2)
+        finish_z(1, 3, 1)
+        finish_n(1, 3, 1)
+        squash(1, 3, 1)
+        store(1, 3, 1)

@@ -14,6 +14,7 @@ FP8 = mybir.dt.float8_e4m3fn
 FP8X4 = mybir.dt.float8_e4m3fn_x4
 ACT = mybir.ActivationFunctionType
 ALU = mybir.AluOpType
+AX = mybir.AxisListType
 
 GZ = 3
 GM = 2
@@ -29,6 +30,8 @@ def tile_legendrememoryunitstep_w8_kernel(
         zwords = ctx.enter_context(tc.tile_pool(name="zwords", bufs=4))
         mrows = ctx.enter_context(tc.tile_pool(name="mrows", bufs=4))
         mwords = ctx.enter_context(tc.tile_pool(name="mwords", bufs=4))
+        nrows = ctx.enter_context(tc.tile_pool(name="nrows", bufs=6))
+        small = ctx.enter_context(tc.tile_pool(name="small", bufs=2))
         results = ctx.enter_context(tc.tile_pool(name="results", bufs=8))
         psum = ctx.enter_context(tc.psum_pool(name="psum", bufs=8))
         ctx.enter_context(tc.manual_schedule())
@@ -39,13 +42,19 @@ def tile_legendrememoryunitstep_w8_kernel(
 
         ident = keep.tile([128, 128], F32, name="ident")
         warm = keep.tile([128, 1], F32, name="warm")
+        ones = keep.tile([128, 512], BF16, name="ones")
         ez_col = keep.tile([128, GZ, 4], BF16, name="ez_col")
-        b_col = keep.tile([128, GM, 4], BF16, name="b_col")
+        b_row = keep.tile([128, P], BF16, name="b_row")
+        b_bc = keep.tile([128, GM, 512], BF16, name="b_bc")
+        same_t = keep.tile([128, 4], F32, name="same_t")
+        row_of = keep.tile([128, 32], F32, name="row_of")
+        gather = keep.tile([128, 4, 32], F32, name="gather")
+        quad = keep.tile([128, 4], F32, name="quad")
+        quad_t = keep.tile([128, 4, 4], F32, name="quad_t")
+        u_col = keep.tile([128, 2, 4], F32, name="u_col")
         m_fac = keep.tile([128, GM, 4], F32, name="m_fac")
         m_raw = keep.tile([128, 2, 4096], U8, name="m_raw")
-        at_raw = keep.tile([128, GM, P], I32, name="at_raw", align_bytes=64)
         at_c = keep.tile([128, GM, P], I32, name="at_c", align_bytes=64)
-        at_sraw = keep.tile([128, P], U8, name="at_sraw", align_bytes=64)
         at_s = keep.tile([128, P], U8, name="at_s", align_bytes=64)
         wz_c = keep.tile([128, GZ, H], I32, name="wz_c", align_bytes=64)
         wz_s = keep.tile([128, H], U8, name="wz_s", align_bytes=64)
@@ -57,8 +66,6 @@ def tile_legendrememoryunitstep_w8_kernel(
         m_g = keep.tile([128, 2, GM, 2048], BF16, name="m_g", align_bytes=64)
         m_c = keep.tile([128, 2, GM, 512], I32, name="m_c", align_bytes=64)
         m_s = keep.tile([128, 2, GM, 512], U8, name="m_s", align_bytes=64)
-        u_bc = keep.tile([128, 2, 512], F32, name="u_bc")
-        n_p = keep.tile([128, 2, GM, 4, 512], BF16, name="n_p")
         n_g = keep.tile([128, 2, GM, 2048], BF16, name="n_g", align_bytes=64)
         n_c = keep.tile([128, 2, GM, 512], I32, name="n_c", align_bytes=64)
         n_s = keep.tile([128, 2, GM, 512], U8, name="n_s", align_bytes=64)
@@ -66,6 +73,7 @@ def tile_legendrememoryunitstep_w8_kernel(
         zpre = {}
         m_bf = {}
         m_pre = {}
+        n_rows = {}
         banks = {}
 
         def load_z(h, r, lo=0, hi=K):
@@ -79,7 +87,29 @@ def tile_legendrememoryunitstep_w8_kernel(
 
         def warm_up():
             bank = psum.tile([128, 512], F32, name="bank")
-            nc.tensor.matmul(bank[:], lhsT=zeros[:, 0:128], rhs=zeros[:], start=True, stop=True)
+            nc.tensor.matmul(bank[:], lhsT=ones[:, 0:128], rhs=ones[:], start=True, stop=True)
+
+        def make_masks():
+            nc.vector.tensor_reduce(out=same_t[:], in_=ident[:].rearrange("p (j t) -> p t j", t=4), axis=AX.X, op=ALU.add)
+            nc.vector.tensor_reduce(out=row_of[:], in_=ident[:].rearrange("p (j t) -> p j t", t=4), axis=AX.X, op=ALU.add)
+            nc.vector.tensor_reduce(out=quad[:], in_=ident[:].rearrange("p (b i) -> p b i", b=4), axis=AX.X, op=ALU.add)
+            nc.vector.tensor_copy(out=gather[:], in_=row_of[:].unsqueeze(1).to_broadcast([128, 4, 32]))
+            nc.vector.tensor_copy(out=quad_t[:], in_=quad[:].unsqueeze(2).to_broadcast([128, 4, 4]))
+
+        def load_b():
+            nc.sync.dma_start(out=b_row[0:1, :], in_=bvec.rearrange("(o n) -> o n", o=1))
+
+        def spread_b(c):
+            bank = psum.tile([128, 512], F32, name="bank")
+            nc.tensor.matmul(bank[:], lhsT=ones[:, 0:128], rhs=b_row[:, c * 512 : (c + 1) * 512], start=True, stop=True)
+            banks[("b", c)] = bank
+
+        def take_b(c, engine="s"):
+            copy = nc.vector.tensor_copy if engine == "v" else nc.scalar.copy
+            copy(
+                out=b_bc[:, c, :].rearrange("p (u x e) -> p u x e", u=2, e=2),
+                in_=banks[("b", c)][:].rearrange("p (x u e) -> p u x e", u=2, e=2),
+            )
 
         def load_m(h, q):
             cols = slice(q * 2048, (q + 1) * 2048)
@@ -127,25 +157,58 @@ def tile_legendrememoryunitstep_w8_kernel(
                 in_=bank[:].rearrange("p (u c) -> p c u", u=2),
             )
 
-        def quant(src, codes, scales, h, g):
-            nc.vector.quantize_mx(out=codes[:, h, g, :].bitcast(FP8X4), scales=scales[:, h, g, :], in_=src[:, h, g, :])
+        def quant(src, codes, scales, h, q, g):
+            cols = slice(q * 256, (q + 1) * 256)
+            nc.vector.quantize_mx(
+                out=codes[:, h, g, cols].bitcast(FP8X4),
+                scales=scales[:, h, g, cols],
+                in_=src[:, h, g, q * 1024 : (q + 1) * 1024],
+            )
 
-        def write_scalar(h, q, g):
-            if g == 0:
-                bank = psum.tile([128, 512], F32, name="bank")
-                banks[("u", h, q)] = bank
-            for t in range(4):
-                nc.tensor.matmul(
-                    banks[("u", h, q)][:, 0:256],
-                    lhsT=ez_col[:, g, t : t + 1].to_broadcast([128, 128]),
-                    rhs=z_g[:, h, g, q * 1024 : (q + 1) * 1024].rearrange("p (c t) -> p t c", t=4)[:, t, :],
-                    start=(g == 0 and t == 0),
-                    stop=(g == GZ - 1 and t == 3),
-                )
+        def write_scalar(h, q):
+            bank = psum.tile([128, 512], F32, name="bank")
+            for x in range(8):
+                for g in range(GZ):
+                    lo = q * 1024 + x * 128
+                    nc.tensor.matmul(
+                        bank[:, 4 * x : 4 * x + 4],
+                        lhsT=z_g[:, h, g, lo : lo + 128],
+                        rhs=ez_col[:, g, :],
+                        start=(g == 0),
+                        stop=(g == GZ - 1),
+                    )
+            banks[("u", h, q)] = bank
 
-        def take_scalar(h, q, engine="s"):
-            copy = nc.vector.tensor_copy if engine == "v" else nc.scalar.copy
-            copy(out=u_bc[:, h, q * 256 : (q + 1) * 256], in_=banks[("u", h, q)][:, 0:256])
+        def pick_products(h, q):
+            prod = small.tile([128, 8, 4], F32, name="prod")
+            nc.vector.tensor_tensor(
+                out=prod[:],
+                in0=banks[("u", h, q)][:, 0:32].rearrange("p (x t) -> p x t", t=4),
+                in1=same_t[:].unsqueeze(1).to_broadcast([128, 8, 4]),
+                op=ALU.mult,
+            )
+            banks[("prod", h, q)] = prod
+
+        def gather_scalar(h, q):
+            bank = psum.tile([128, 512], F32, name="bank")
+            nc.tensor.matmul(
+                bank[:, 0:32],
+                lhsT=gather[:].rearrange("p b j -> p (b j)"),
+                rhs=banks[("prod", h, q)][:].rearrange("p x t -> p (x t)"),
+                start=True,
+                stop=True,
+            )
+            banks[("w", h, q)] = bank
+
+        def take_scalar(h, q):
+            part = small.tile([128, 2, 16], F32, name="part")
+            nc.vector.tensor_tensor(
+                out=part[:],
+                in0=banks[("w", h, q)][:, 0:32].rearrange("p (j x) -> p j x", j=2),
+                in1=quad_t[:].rearrange("p b t -> p (b t)").unsqueeze(1).to_broadcast([128, 2, 16]),
+                op=ALU.mult,
+            )
+            nc.vector.tensor_reduce(out=u_col[:, h, 2 * q : 2 * q + 2], in_=part[:], axis=AX.X, op=ALU.add)
 
         def cast_m(h, r, engine="s"):
             mt = mrows.tile([128, 1024], BF16, name="mt")
@@ -187,52 +250,55 @@ def tile_legendrememoryunitstep_w8_kernel(
                 op=ALU.mult,
             )
 
-        def order_at(g):
-            nc.vector.tensor_copy(
-                out=at_c[:, g, :].rearrange("p (k t c) -> p k c t", t=4, c=128),
-                in_=at_raw[:, g, :].rearrange("p (k c t) -> p k c t", t=4, c=128),
-            )
-
-        def order_at_scales(engine="v"):
-            copy = nc.vector.tensor_copy if engine == "v" else nc.gpsimd.tensor_copy
-            copy(
-                out=at_s[:].rearrange("p (k t c) -> p k c t", t=4, c=128),
-                in_=at_sraw[:].rearrange("p (k c t) -> p k c t", t=4, c=128),
-            )
-
-        def memory(h, k, t):
+        def memory(h, r, c):
             bank = psum.tile([128, 512], F32, name="bank")
-            lo = k * 512 + t * 128
+            rows = slice(r * 128, (r + 1) * 128)
+            cols = slice(c * 512, (c + 1) * 512)
             for g in range(GM):
                 nc.tensor.matmul_mx(
                     out=bank[:],
-                    lhsT=at_c[:, g, lo : lo + 128].bitcast(FP8X4),
-                    lhsT_scale=at_s[4 * g : 128, lo : lo + 128],
-                    rhs=m_c[:, h, g, :].bitcast(FP8X4),
-                    rhs_scale=m_s[:, h, g, :],
+                    lhsT=m_c[:, h, g, rows].bitcast(FP8X4),
+                    lhsT_scale=m_s[:, h, g, rows],
+                    rhs=at_c[:, g, cols].bitcast(FP8X4),
+                    rhs_scale=at_s[4 * g : 128, cols],
                     start=(g == 0),
                     stop=(g == GM - 1),
                 )
-            banks[("n", h, k, t)] = bank
+            banks[("n", h, r, c)] = bank
 
-        def take_memory(h, k, t):
-            bank = banks[("n", h, k, t)]
-            nc.vector.scalar_tensor_tensor(
-                out=n_p[:, h, k, t, :],
-                in0=u_bc[:, h, :],
-                scalar=b_col[:, k, t : t + 1],
-                in1=bank[:],
-                op0=ALU.mult,
-                op1=ALU.add,
+        def take_memory(h, r, c):
+            if (h, r) not in n_rows:
+                nr = nrows.tile([128, 1024], BF16, name="nr")
+                n_rows[(h, r)] = nr
+            for u in range(2):
+                lo = c * 512 + u * 256
+                nc.vector.scalar_tensor_tensor(
+                    out=n_rows[(h, r)][:, lo : lo + 256].rearrange("p (x e) -> p x e", e=2),
+                    in0=b_bc[:, c, u * 256 : (u + 1) * 256].rearrange("p (x e) -> p x e", e=2),
+                    scalar=u_col[:, h, r : r + 1],
+                    in1=banks[("n", h, r, c)][:].rearrange("p (x u e) -> p u x e", u=2, e=2)[:, u],
+                    op0=ALU.mult,
+                    op1=ALU.add,
+                )
+
+        def turn_n(h, q, g):
+            bank = psum.tile([128, 512], F32, name="bank")
+            for j in range(2):
+                words = n_rows[(h, 2 * q + j)][:].bitcast(F32)
+                for u in range(2):
+                    nc.tensor.transpose(
+                        bank[:, u * 256 + j * 128 : u * 256 + (j + 1) * 128],
+                        words[:, g * 256 + u * 128 : g * 256 + (u + 1) * 128],
+                        ident[:],
+                    )
+            banks[("t", h, q, g)] = bank
+
+        def take_n(h, q, g, engine="s"):
+            copy = nc.vector.tensor_copy if engine == "v" else nc.scalar.copy
+            copy(
+                out=n_g[:, h, g, q * 1024 : (q + 1) * 1024].bitcast(F32),
+                in_=banks[("t", h, q, g)][:].rearrange("p (u c) -> p c u", u=2),
             )
-
-        def interleave(h, k, engine):
-            dst = n_g[:, h, k, :].rearrange("p (c t) -> p c t", t=4)
-            src = n_p[:, h, k, :, :].rearrange("p t c -> p c t")
-            if engine == "v":
-                nc.vector.tensor_copy(out=dst, in_=src)
-            else:
-                nc.scalar.copy(out=dst, in_=src)
 
         def finish_z(h, r, c):
             bank = psum.tile([128, 512], F32, name="bank")
@@ -279,243 +345,267 @@ def tile_legendrememoryunitstep_w8_kernel(
 
         make_identity(nc, ident[:])
         nc.vector.memset(warm[:], 0.0)
-        zeros = keep.tile([128, 512], BF16, name="zeros")
-        nc.vector.memset(zeros[:], 0.0)
-        nc.vector.memset(at_sraw[:].bitcast(I32), 0)
+        nc.vector.memset(ones[:], 1.0)
+        nc.vector.memset(b_row[:], 0.0)
+        nc.vector.memset(at_s[:].bitcast(I32), 0)
         nc.vector.memset(wz_s[:].bitcast(I32), 0)
         nc.vector.memset(wm_s[:].bitcast(I32), 0)
         nc.scalar.activation(out=warm[:], in_=warm[:], func=ACT.Tanh)
+        warm_up()
+        make_masks()
+        warm_up()
+        warm_up()
         load_m(0, 1)
-        cast_m(0, 3, "s")
-        warm_up()
-        warm_up()
-        warm_up()
-        load_small(ez_col, ez.rearrange("(g p t) -> p g t", p=128, t=4))
-        warm_up()
-        warm_up()
-        cast_m(0, 2, "v")
+        cast_m(0, 3, "v")
+        cast_m(0, 2, "s")
+        turn_m(0, 1, 0)
+        turn_m(0, 1, 1)
         load_m(0, 0)
         cast_m(0, 0, "v")
-        cast_m(0, 1, "v")
-        warm_up()
-        load_small(m_fac, m_scale.rearrange("o (g p t) -> p (o g) t", p=128, t=4))
-        turn_m(0, 1, 0)
-        take_m(0, 1, 0)
         warm_up()
         load_m(1, 0)
         cast_m(1, 0, "s")
         cast_m(1, 1, "s")
-        pre_m(1, 0, "s")
-        pre_m(1, 1, "s")
-        load_z(0, 3)
         warm_up()
-        turn_m(0, 0, 1)
-        load_z(0, 0, 0, 512)
-        take_m(0, 0, 1)
+        cast_m(0, 1, "v")
         turn_m(0, 0, 0)
-        load_z(0, 1, 0, 512)
-        turn_z(0, 0, 0, direct=True)
-        take_z(0, 0, 0, "s")
-        warm_up()
-        load_small(b_col, bvec.rearrange("(g p t) -> p g t", p=128, t=4))
-        warm_up()
+        load_small(m_fac, m_scale.rearrange("o (g p t) -> p (o g) t", p=128, t=4))
+        take_m(0, 1, 0)
+        take_m(0, 1, 1)
+        quant(m_g, m_c, m_s, 0, 1, 0)
         take_m(0, 0, 0)
-        quant(m_g, m_c, m_s, 0, 0)
-        load_z(0, 2)
-        turn_z(0, 1, 0, direct=True)
-        take_z(0, 1, 0, "s")
-        turn_z(0, 1, 2, direct=True)
-        turn_z(0, 1, 1, direct=True)
-        write_scalar(0, 1, 0)
-        take_z(0, 1, 2, "s")
-        take_z(0, 1, 1, "s")
-        quant(z_g, z_c, z_s, 0, 0)
-        load_z(0, 1, 512, K)
-        load_scales(at_sraw, at_scales, GM)
-        order_at_scales("v")
-        load_z(1, 0)
-        pre_z(1, 0, "s")
-        turn_m(1, 0, 0)
-        take_m(1, 0, 0)
-        load_z(0, 0, 512, K)
-        turn_z(0, 0, 1, direct=True)
-        take_z(0, 0, 1, "s")
-        load_words(at_raw, at_words, 0)
-        order_at(0)
-        turn_z(0, 0, 2, direct=True)
-        take_z(0, 0, 2, "s")
-        quant(z_g, z_c, z_s, 0, 2)
-        write_scalar(0, 1, 1)
-        write_scalar(0, 1, 2)
-        take_scalar(0, 1, "s")
-        write_scalar(0, 0, 0)
-        write_scalar(0, 0, 1)
-        turn_m(0, 1, 1)
-        load_z(1, 1)
-        pre_z(1, 1, "s")
-        turn_z(1, 0, 0)
-        take_z(1, 0, 0, "s")
-        turn_z(1, 0, 1)
-        take_z(1, 0, 1, "s")
-        turn_z(1, 0, 2)
-        take_z(1, 0, 2, "s")
-        write_scalar(0, 0, 2)
-        take_scalar(0, 0, "s")
-        load_scales(wm_s, wm_scales, GM)
-        quant(z_g, z_c, z_s, 0, 1)
+        load_z(0, 0)
+        load_b()
+        spread_b(1)
+        take_b(1, "v")
+        pre_m(1, 0, "s")
         load_z(1, 3)
         pre_z(1, 3, "s")
-        write_scalar(1, 0, 0)
-        write_scalar(1, 0, 1)
-        write_scalar(1, 0, 2)
-        take_scalar(1, 0, "s")
-        take_m(0, 1, 1)
-        quant(m_g, m_c, m_s, 0, 1)
-        load_words(wm_c, wm_words, 0)
-        load_words(at_raw, at_words, 1)
-        order_at(1)
-        memory(0, 0, 3)
-        take_memory(0, 0, 3)
-        memory(0, 0, 1)
-        take_memory(0, 0, 1)
-        memory(0, 1, 1)
-        take_memory(0, 1, 1)
-        memory(0, 0, 0)
-        take_memory(0, 0, 0)
-        memory(0, 1, 0)
-        take_memory(0, 1, 0)
-        memory(0, 1, 2)
-        take_memory(0, 1, 2)
-        memory(0, 0, 2)
-        take_memory(0, 0, 2)
-        interleave(0, 0, "v")
-        memory(0, 1, 3)
-        take_memory(0, 1, 3)
-        quant(n_g, n_c, n_s, 0, 0)
-        interleave(0, 1, "v")
-        quant(n_g, n_c, n_s, 0, 1)
-        load_m(1, 1)
-        cast_m(1, 2, "s")
-        pre_m(1, 2, "s")
-        cast_m(1, 3, "s")
-        load_words(wz_c, wz_words, 1)
+        load_z(1, 1)
+        pre_z(1, 1, "s")
+        load_z(0, 1)
+        turn_z(0, 0, 2, direct=True)
+        take_z(0, 0, 2, "s")
+        quant(z_g, z_c, z_s, 0, 0, 2)
+        turn_z(0, 0, 1, direct=True)
+        turn_z(0, 0, 0, direct=True)
+        take_z(0, 0, 0, "s")
+        quant(z_g, z_c, z_s, 0, 0, 0)
+        take_z(0, 0, 1, "s")
+        pre_m(1, 1, "v")
+        turn_m(0, 0, 1)
+        take_m(0, 0, 1)
+        load_z(0, 3)
+        warm_up()
+        quant(m_g, m_c, m_s, 0, 1, 1)
+        load_z(0, 2)
+        turn_z(0, 1, 1, direct=True)
+        take_z(0, 1, 1, "s")
+        quant(z_g, z_c, z_s, 0, 1, 1)
+        turn_z(0, 1, 2, direct=True)
+        take_z(0, 1, 2, "s")
+        quant(z_g, z_c, z_s, 0, 1, 2)
+        turn_z(0, 1, 0, direct=True)
+        turn_m(1, 0, 0)
+        take_m(1, 0, 0)
+        load_small(ez_col, ez.rearrange("(g p t) -> p g t", p=128, t=4))
+        write_scalar(0, 0)
+        pick_products(0, 0)
+        load_words(at_c, at_words, 0)
+        take_z(0, 1, 0, "s")
+        write_scalar(0, 1)
+        pick_products(0, 1)
+        quant(m_g, m_c, m_s, 0, 0, 1)
+        load_words(at_c, at_words, 1)
+        quant(m_g, m_c, m_s, 0, 0, 0)
         load_z(1, 2)
         pre_z(1, 2, "s")
         turn_z(1, 1, 0)
-        take_z(1, 1, 0, "s")
-        turn_z(1, 1, 1)
-        turn_z(1, 1, 2)
+        take_z(1, 1, 0, "v")
+        spread_b(0)
+        take_b(0, "v")
+        load_z(1, 0)
+        pre_z(1, 0, "s")
+        turn_z(1, 0, 2)
+        turn_z(1, 0, 1)
+        take_z(1, 0, 2, "s")
+        take_z(1, 0, 1, "s")
+        quant(z_g, z_c, z_s, 1, 0, 2)
+        turn_z(1, 0, 0)
+        take_z(1, 0, 0, "s")
+        warm_up()
+        quant(z_g, z_c, z_s, 1, 1, 0)
+        gather_scalar(0, 1)
+        take_scalar(0, 1)
+        gather_scalar(0, 0)
+        take_scalar(0, 0)
         load_words(wz_c, wz_words, 0)
         turn_m(1, 0, 1)
         take_m(1, 0, 1)
-        load_scales(wz_s, wz_scales, GZ)
-        write_scalar(1, 1, 0)
+        turn_z(1, 1, 2)
+        take_z(1, 1, 2, "s")
+        load_m(1, 1)
+        cast_m(1, 3, "s")
+        cast_m(1, 2, "s")
         pre_m(1, 3, "s")
-        turn_m(1, 1, 0)
-        take_m(1, 1, 0)
+        pre_m(1, 2, "s")
+        load_scales(wm_s, wm_scales, GM)
+        load_words(wz_c, wz_words, 2)
+        write_scalar(1, 0)
+        pick_products(1, 0)
+        load_scales(at_s, at_scales, GM)
+        memory(0, 0, 0)
+        memory(0, 1, 0)
+        memory(0, 1, 1)
+        take_memory(0, 0, 0)
+        take_memory(0, 1, 0)
+        memory(0, 2, 0)
+        memory(0, 2, 1)
+        take_memory(0, 1, 1)
+        take_memory(0, 2, 0)
+        take_memory(0, 2, 1)
+        memory(0, 0, 1)
+        take_memory(0, 0, 1)
+        memory(0, 3, 1)
+        take_memory(0, 3, 1)
+        turn_z(1, 1, 1)
+        take_z(1, 1, 1, "s")
+        memory(0, 3, 0)
+        take_memory(0, 3, 0)
+        load_words(wm_c, wm_words, 0)
+        gather_scalar(1, 0)
+        take_scalar(1, 0)
+        load_words(wz_c, wz_words, 1)
+        turn_n(0, 0, 0)
+        take_n(0, 0, 0, "s")
+        write_scalar(1, 1)
+        pick_products(1, 1)
+        warm_up()
+        quant(z_g, z_c, z_s, 0, 0, 1)
+        turn_n(0, 0, 1)
+        quant(n_g, n_c, n_s, 0, 0, 0)
+        turn_n(0, 1, 1)
+        take_n(0, 1, 1, "s")
+        quant(n_g, n_c, n_s, 0, 1, 1)
         turn_m(1, 1, 1)
         take_m(1, 1, 1)
-        quant(m_g, m_c, m_s, 1, 1)
+        take_n(0, 0, 1, "s")
+        quant(n_g, n_c, n_s, 0, 0, 1)
+        quant(m_g, m_c, m_s, 1, 0, 1)
+        quant(z_g, z_c, z_s, 1, 0, 0)
+        turn_n(0, 1, 0)
+        take_n(0, 1, 0, "s")
+        quant(n_g, n_c, n_s, 0, 1, 0)
+        quant(z_g, z_c, z_s, 0, 1, 0)
         load_words(wm_c, wm_words, 1)
-        take_z(1, 1, 1, "s")
-        quant(z_g, z_c, z_s, 1, 1)
-        write_scalar(1, 1, 1)
-        take_z(1, 1, 2, "s")
-        write_scalar(1, 1, 2)
-        quant(z_g, z_c, z_s, 1, 2)
-        take_scalar(1, 1, "s")
-        load_words(wz_c, wz_words, 2)
-        finish_z(0, 3, 0)
-        finish_z(0, 1, 0)
-        finish_z(0, 0, 0)
-        finish_n(0, 0, 0)
-        squash(0, 0, 0)
-        store(0, 0, 0)
-        finish_z(0, 2, 1)
-        finish_n(0, 2, 1)
+        turn_m(1, 1, 0)
+        take_m(1, 1, 0)
+        quant(m_g, m_c, m_s, 1, 1, 0)
+        quant(z_g, z_c, z_s, 1, 1, 2)
+        gather_scalar(1, 1)
+        take_scalar(1, 1)
+        load_scales(wz_s, wz_scales, GZ)
         finish_z(0, 0, 1)
-        squash(0, 2, 1)
-        store(0, 2, 1)
+        finish_z(0, 0, 0)
+        finish_z(0, 1, 1)
+        finish_n(0, 1, 1)
+        finish_z(0, 1, 0)
         finish_n(0, 1, 0)
         squash(0, 1, 0)
         store(0, 1, 0)
+        squash(0, 1, 1)
+        store(0, 1, 1)
+        finish_z(0, 3, 1)
+        finish_n(0, 3, 1)
+        squash(0, 3, 1)
+        store(0, 3, 1)
+        finish_n(0, 0, 0)
+        squash(0, 0, 0)
+        store(0, 0, 0)
         finish_n(0, 0, 1)
-        finish_n(0, 3, 0)
-        squash(0, 3, 0)
-        store(0, 3, 0)
         squash(0, 0, 1)
         store(0, 0, 1)
-        quant(m_g, m_c, m_s, 1, 0)
-        memory(1, 1, 3)
-        take_memory(1, 1, 3)
-        memory(1, 1, 0)
-        take_memory(1, 1, 0)
-        memory(1, 1, 2)
-        take_memory(1, 1, 2)
-        memory(1, 0, 3)
-        take_memory(1, 0, 3)
-        memory(1, 0, 2)
-        take_memory(1, 0, 2)
+        quant(m_g, m_c, m_s, 1, 1, 1)
+        memory(1, 3, 0)
+        take_memory(1, 3, 0)
+        memory(1, 2, 0)
+        take_memory(1, 2, 0)
+        memory(1, 2, 1)
+        take_memory(1, 2, 1)
+        memory(1, 3, 1)
+        take_memory(1, 3, 1)
+        finish_z(0, 2, 1)
+        finish_n(0, 2, 1)
+        squash(0, 2, 1)
+        store(0, 2, 1)
+        finish_z(0, 2, 0)
+        finish_n(0, 2, 0)
+        squash(0, 2, 0)
+        store(0, 2, 0)
+        quant(m_g, m_c, m_s, 1, 0, 0)
         memory(1, 1, 1)
         take_memory(1, 1, 1)
         memory(1, 0, 1)
         take_memory(1, 0, 1)
         memory(1, 0, 0)
         take_memory(1, 0, 0)
-        interleave(1, 0, "v")
-        interleave(1, 1, "s")
-        quant(n_g, n_c, n_s, 1, 1)
-        quant(n_g, n_c, n_s, 1, 0)
-        finish_z(0, 3, 1)
-        finish_n(0, 3, 1)
-        squash(0, 3, 1)
-        store(0, 3, 1)
-        finish_z(0, 2, 0)
-        finish_n(0, 2, 0)
-        squash(0, 2, 0)
-        store(0, 2, 0)
-        finish_z(0, 1, 1)
-        finish_n(0, 1, 1)
-        squash(0, 1, 1)
-        store(0, 1, 1)
-        quant(z_g, z_c, z_s, 1, 0)
+        memory(1, 1, 0)
+        take_memory(1, 1, 0)
+        turn_n(1, 1, 0)
+        take_n(1, 1, 0, "s")
+        quant(n_g, n_c, n_s, 1, 1, 0)
+        finish_z(0, 3, 0)
+        finish_n(0, 3, 0)
+        squash(0, 3, 0)
+        store(0, 3, 0)
+        turn_n(1, 1, 1)
+        turn_n(1, 0, 0)
+        take_n(1, 0, 0, "s")
+        turn_n(1, 0, 1)
+        quant(z_g, z_c, z_s, 1, 0, 1)
+        finish_z(1, 1, 0)
         finish_z(1, 0, 0)
+        finish_z(1, 1, 1)
+        finish_z(1, 0, 1)
+        take_n(1, 1, 1, "v")
+        quant(n_g, n_c, n_s, 1, 1, 1)
+        quant(n_g, n_c, n_s, 1, 0, 0)
+        take_n(1, 0, 1, "s")
+        quant(n_g, n_c, n_s, 1, 0, 1)
+        finish_n(1, 0, 1)
+        squash(1, 0, 1)
         finish_n(1, 0, 0)
+        finish_n(1, 1, 1)
+        squash(1, 0, 0)
+        store(1, 0, 0)
+        store(1, 0, 1)
+        squash(1, 1, 1)
+        store(1, 1, 1)
+        finish_n(1, 1, 0)
+        squash(1, 1, 0)
+        store(1, 1, 0)
+        quant(z_g, z_c, z_s, 1, 1, 1)
+        finish_z(1, 2, 0)
         finish_z(1, 2, 1)
+        finish_n(1, 2, 0)
+        finish_z(1, 3, 1)
+        finish_n(1, 3, 1)
+        finish_n(1, 2, 1)
+        squash(1, 3, 1)
+        store(1, 3, 1)
+        squash(1, 2, 1)
+        store(1, 2, 1)
+        finish_z(1, 3, 3)
+        squash(1, 2, 0)
+        store(1, 2, 0)
+        finish_n(1, 3, 3)
+        squash(1, 3, 3)
+        store(1, 3, 3)
         finish_z(1, 3, 0)
         finish_n(1, 3, 0)
         squash(1, 3, 0)
         store(1, 3, 0)
-        finish_z(1, 2, 0)
-        finish_z(1, 0, 1)
-        finish_n(1, 0, 1)
-        squash(1, 0, 1)
-        store(1, 0, 1)
-        squash(1, 0, 0)
-        store(1, 0, 0)
-        finish_n(1, 2, 0)
-        squash(1, 2, 0)
-        finish_z(1, 1, 0)
-        finish_n(1, 1, 0)
-        squash(1, 1, 0)
-        store(1, 1, 0)
-        store(1, 2, 0)
-        finish_z(1, 1, 1)
-        finish_n(1, 1, 1)
-        squash(1, 1, 1)
-        store(1, 1, 1)
-        finish_n(1, 2, 1)
-        squash(1, 2, 1)
-        store(1, 2, 1)
-        finish_z(1, 3, 3)
-        finish_n(1, 3, 3)
-        squash(1, 3, 3)
-        store(1, 3, 3)
         finish_z(1, 3, 2)
         finish_n(1, 3, 2)
         squash(1, 3, 2)
         store(1, 3, 2)
-        finish_z(1, 3, 1)
-        finish_n(1, 3, 1)
-        squash(1, 3, 1)
-        store(1, 3, 1)

@@ -4,7 +4,7 @@ import concourse.mybir as mybir
 from concourse.masks import make_identity
 
 N, K, P, H = 1024, 1536, 1024, 1024
-FLOPS = 2 * N * H * (K + P) + 2 * N * P * P
+FLOPS = 2 * N * P * P + 2 * N * (K + P) * H
 
 F32 = mybir.dt.float32
 BF16 = mybir.dt.bfloat16
@@ -16,22 +16,24 @@ ACT = mybir.ActivationFunctionType
 ALU = mybir.AluOpType
 AX = mybir.AxisListType
 
-GZ = 3
-GM = 2
+GZ = K // 512
+GM = P // 512
 
 
 def tile_legendrememoryunitstep_w8_kernel(
     tc, z, m_bytes, m_scale, ez, at_words, at_scales, bvec, wz_words, wz_scales, wm_words, wm_scales, out
 ):
     nc = tc.nc
+    on_vector = nc.vector.tensor_copy
+    on_scalar = nc.scalar.copy
+
     with ExitStack() as ctx:
         keep = ctx.enter_context(tc.tile_pool(name="keep", bufs=1))
-        stage = ctx.enter_context(tc.tile_pool(name="stage", bufs=8))
-        zwords = ctx.enter_context(tc.tile_pool(name="zwords", bufs=4))
+        zrows = ctx.enter_context(tc.tile_pool(name="zrows", bufs=8))
+        words_pool = ctx.enter_context(tc.tile_pool(name="words", bufs=4))
         mrows = ctx.enter_context(tc.tile_pool(name="mrows", bufs=4))
-        mwords = ctx.enter_context(tc.tile_pool(name="mwords", bufs=4))
-        nrows = ctx.enter_context(tc.tile_pool(name="nrows", bufs=6))
-        small = ctx.enter_context(tc.tile_pool(name="small", bufs=2))
+        nrows = ctx.enter_context(tc.tile_pool(name="nrows", bufs=8))
+        small = ctx.enter_context(tc.tile_pool(name="small", bufs=4))
         results = ctx.enter_context(tc.tile_pool(name="results", bufs=8))
         psum = ctx.enter_context(tc.psum_pool(name="psum", bufs=8))
         ctx.enter_context(tc.manual_schedule())
@@ -41,19 +43,21 @@ def tile_legendrememoryunitstep_w8_kernel(
         out_rows = out.rearrange("(h p r) c -> h p r c", h=2, p=128)
 
         ident = keep.tile([128, 128], F32, name="ident")
-        warm = keep.tile([128, 1], F32, name="warm")
         ones = keep.tile([128, 512], BF16, name="ones")
+        table = keep.tile([128, 1], F32, name="table")
         ez_col = keep.tile([128, GZ, 4], BF16, name="ez_col")
+        m_fac = keep.tile([128, GM, 4], F32, name="m_fac")
+        m_raw = keep.tile([128, 2, 4 * P], U8, name="m_raw")
         b_row = keep.tile([128, P], BF16, name="b_row")
-        b_bc = keep.tile([128, GM, 512], BF16, name="b_bc")
+        b_all = keep.tile([128, GM, 512], BF16, name="b_all")
+
         same_t = keep.tile([128, 4], F32, name="same_t")
         row_of = keep.tile([128, 32], F32, name="row_of")
         gather = keep.tile([128, 4, 32], F32, name="gather")
-        quad = keep.tile([128, 4], F32, name="quad")
-        quad_t = keep.tile([128, 4, 4], F32, name="quad_t")
+        block_of = keep.tile([128, 4], F32, name="block_of")
+        block_t = keep.tile([128, 4, 4], F32, name="block_t")
         u_col = keep.tile([128, 2, 4], F32, name="u_col")
-        m_fac = keep.tile([128, GM, 4], F32, name="m_fac")
-        m_raw = keep.tile([128, 2, 4096], U8, name="m_raw")
+
         at_c = keep.tile([128, GM, P], I32, name="at_c", align_bytes=64)
         at_s = keep.tile([128, P], U8, name="at_s", align_bytes=64)
         wz_c = keep.tile([128, GZ, H], I32, name="wz_c", align_bytes=64)
@@ -69,107 +73,148 @@ def tile_legendrememoryunitstep_w8_kernel(
         n_g = keep.tile([128, 2, GM, 2048], BF16, name="n_g", align_bytes=64)
         n_c = keep.tile([128, 2, GM, 512], I32, name="n_c", align_bytes=64)
         n_s = keep.tile([128, 2, GM, 512], U8, name="n_s", align_bytes=64)
-        zin = {}
-        zpre = {}
-        m_bf = {}
-        m_pre = {}
-        n_rows = {}
-        banks = {}
+
+        z_in, z_words, m_in, m_words, n_in, banks = {}, {}, {}, {}, {}, {}
 
         def load_z(h, r, lo=0, hi=K):
-            if (h, r) not in zin:
-                zt = stage.tile([128, K], BF16, name="zt")
-                zin[(h, r)] = zt
-            nc.sync.dma_start(out=zin[(h, r)][:, lo:hi], in_=z_rows[h][:, r, lo:hi])
+            if (h, r) not in z_in:
+                zt = zrows.tile([128, K], BF16, name="zt")
+                z_in[(h, r)] = zt
+            nc.sync.dma_start(out=z_in[(h, r)][:, lo:hi], in_=z_rows[h][:, r, lo:hi])
 
-        def load_small(tile, src):
-            nc.sync.dma_start(out=tile[:], in_=src)
+        def load_m(h, first, end):
+            cols = slice(first * P, end * P)
+            nc.sync.dma_start(out=m_raw[:, h, cols], in_=m_rows[h][:, cols])
 
-        def warm_up():
+        def load_words(codes, words, g):
+            nc.sync.dma_start(out=codes[:, g, :], in_=words[g].rearrange("p n t -> p (n t)").bitcast(I32))
+
+        def load_scales(planes, scales, passes):
+            for quadrant in range(4):
+                nc.sync.dma_start(
+                    out=planes[32 * quadrant : 32 * quadrant + 4 * passes, :].bitcast(I32),
+                    in_=scales[:, 4 * quadrant : 4 * quadrant + 4, :].bitcast(I32),
+                )
+
+        def load_small(dst, src):
+            nc.sync.dma_start(out=dst, in_=src)
+
+        def make_masks():
+            for mask, view in (
+                (same_t, ident[:].rearrange("p (j t) -> p t j", t=4)),
+                (row_of, ident[:].rearrange("p (j t) -> p j t", t=4)),
+                (block_of, ident[:].rearrange("p (b i) -> p b i", b=4)),
+            ):
+                nc.vector.tensor_reduce(out=mask[:], in_=view, axis=AX.X, op=ALU.add)
+            nc.vector.tensor_copy(out=gather[:], in_=row_of[:].unsqueeze(1).to_broadcast([128, 4, 32]))
+            nc.vector.tensor_copy(out=block_t[:], in_=block_of[:].unsqueeze(2).to_broadcast([128, 4, 4]))
+
+        def keep_busy():
             bank = psum.tile([128, 512], F32, name="bank")
             nc.tensor.matmul(bank[:], lhsT=ones[:, 0:128], rhs=ones[:], start=True, stop=True)
 
-        def make_masks():
-            nc.vector.tensor_reduce(out=same_t[:], in_=ident[:].rearrange("p (j t) -> p t j", t=4), axis=AX.X, op=ALU.add)
-            nc.vector.tensor_reduce(out=row_of[:], in_=ident[:].rearrange("p (j t) -> p j t", t=4), axis=AX.X, op=ALU.add)
-            nc.vector.tensor_reduce(out=quad[:], in_=ident[:].rearrange("p (b i) -> p b i", b=4), axis=AX.X, op=ALU.add)
-            nc.vector.tensor_copy(out=gather[:], in_=row_of[:].unsqueeze(1).to_broadcast([128, 4, 32]))
-            nc.vector.tensor_copy(out=quad_t[:], in_=quad[:].unsqueeze(2).to_broadcast([128, 4, 4]))
+        def spread_b():
+            for c in range(GM):
+                bank = psum.tile([128, 512], F32, name="bank")
+                nc.tensor.matmul(
+                    bank[:], lhsT=ones[:, 0:128], rhs=b_row[:, c * 512 : (c + 1) * 512], start=True, stop=True
+                )
+                banks[("b", c)] = bank
 
-        def load_b():
-            nc.sync.dma_start(out=b_row[0:1, :], in_=bvec.rearrange("(o n) -> o n", o=1))
-
-        def spread_b(c):
-            bank = psum.tile([128, 512], F32, name="bank")
-            nc.tensor.matmul(bank[:], lhsT=ones[:, 0:128], rhs=b_row[:, c * 512 : (c + 1) * 512], start=True, stop=True)
-            banks[("b", c)] = bank
-
-        def take_b(c, engine="s"):
-            copy = nc.vector.tensor_copy if engine == "v" else nc.scalar.copy
-            copy(
-                out=b_bc[:, c, :].rearrange("p (u x e) -> p u x e", u=2, e=2),
-                in_=banks[("b", c)][:].rearrange("p (x u e) -> p u x e", u=2, e=2),
-            )
-
-        def load_m(h, q):
-            cols = slice(q * 2048, (q + 1) * 2048)
-            nc.sync.dma_start(out=m_raw[:, h, cols], in_=m_rows[h][:, cols])
-
-        def load_words(tile, words, g):
-            nc.sync.dma_start(out=tile[:, g, :], in_=words[g].rearrange("p n t -> p (n t)").bitcast(I32))
-
-        def load_scales(tile, scales, groups):
-            for q in range(4):
-                nc.sync.dma_start(
-                    out=tile[32 * q : 32 * q + 4 * groups, :].bitcast(I32),
-                    in_=scales[:, 4 * q : 4 * q + 4, :].bitcast(I32),
+        def take_b(copy):
+            for c in range(GM):
+                copy(
+                    out=b_all[:, c, :].rearrange("p (u x e) -> p u x e", u=2, e=2),
+                    in_=banks[("b", c)][:].rearrange("p (x u e) -> p u x e", u=2, e=2),
                 )
 
-        def pre_z(h, r, engine="v"):
-            zp = zwords.tile([128, K // 2], F32, name="zp")
-            copy = nc.vector.tensor_copy if engine == "v" else nc.scalar.copy
-            copy(
-                out=zp[:].rearrange("p (u c) -> p u c", u=2),
-                in_=zin[(h, r)][:].bitcast(F32).rearrange("p (c u) -> p u c", u=2),
-            )
-            zpre[(h, r)] = zp
+        def pair(q):
+            return (2 * q, 2 * q + 1)
 
-        def turn_z(h, q, g, direct=False):
+        def order_words(rows, copy):
+            src = rows[:].bitcast(F32)
+            ordered = words_pool.tile([128, src.shape[1]], F32, name="ordered%d" % src.shape[1])
+            copy(
+                out=ordered[:].rearrange("p (u c) -> p u c", u=2),
+                in_=src.rearrange("p (c u) -> p u c", u=2),
+            )
+            return ordered
+
+        def word_columns(rows, ordered, g, u):
+            if ordered is None:
+                return rows[:].bitcast(F32)[:, 256 * g + u : 256 * (g + 1) : 2]
+            lo = u * (ordered.shape[1] // 2) + 128 * g
+            return ordered[:, lo : lo + 128]
+
+        def turn(columns):
             bank = psum.tile([128, 512], F32, name="bank")
             for j in range(2):
                 for u in range(2):
-                    if direct:
-                        words = zin[(h, 2 * q + j)][:].bitcast(F32)[:, 256 * g + u : 256 * (g + 1) : 2]
-                    else:
-                        words = zpre[(h, 2 * q + j)][:, u * 384 + g * 128 : u * 384 + (g + 1) * 128]
-                    nc.tensor.transpose(
-                        bank[:, u * 256 + j * 128 : u * 256 + (j + 1) * 128],
-                        words,
-                        ident[:],
-                    )
-            banks[("z", h, q, g)] = bank
+                    lo = 256 * u + 128 * j
+                    nc.tensor.transpose(bank[:, lo : lo + 128], columns(j, u), ident[:])
+            return bank
 
-        def take_z(h, q, g, engine="s"):
-            bank = banks[("z", h, q, g)]
-            copy = nc.vector.tensor_copy if engine == "v" else nc.scalar.copy
-            copy(
-                out=z_g[:, h, g, q * 1024 : (q + 1) * 1024].bitcast(F32),
-                in_=bank[:].rearrange("p (u c) -> p c u", u=2),
-            )
+        def take_words(grouped, bank, copy):
+            copy(out=grouped.bitcast(F32), in_=bank[:].rearrange("p (u c) -> p c u", u=2))
 
-        def quant(src, codes, scales, h, q, g):
+        def quantize(grouped, codes, scales, h, q, g):
             cols = slice(q * 256, (q + 1) * 256)
             nc.vector.quantize_mx(
                 out=codes[:, h, g, cols].bitcast(FP8X4),
                 scales=scales[:, h, g, cols],
-                in_=src[:, h, g, q * 1024 : (q + 1) * 1024],
+                in_=grouped[:, h, g, q * 1024 : (q + 1) * 1024],
             )
 
-        def write_scalar(h, q):
+        def order_z(h, q, copy):
+            for r in pair(q):
+                z_words[(h, r)] = order_words(z_in[(h, r)], copy)
+
+        def turn_z(h, q):
+            for g in range(GZ):
+                banks[("z", h, q, g)] = turn(
+                    lambda j, u: word_columns(z_in[(h, 2 * q + j)], z_words.get((h, 2 * q + j)), g, u)
+                )
+
+        def take_z(h, q, copy):
+            for g in range(GZ):
+                take_words(z_g[:, h, g, q * 1024 : (q + 1) * 1024], banks[("z", h, q, g)], copy)
+
+        def quantize_z(h, q):
+            for g in range(GZ):
+                quantize(z_g, z_c, z_s, h, q, g)
+
+        def widen_m(h, q, copy):
+            for r in pair(q):
+                mt = mrows.tile([128, P], BF16, name="mt")
+                copy(out=mt[:], in_=m_raw[:, h, r * P : (r + 1) * P].bitcast(FP8))
+                m_in[(h, r)] = mt
+
+        def order_m(h, q, copy):
+            for r in pair(q):
+                m_words[(h, r)] = order_words(m_in[(h, r)], copy)
+
+        def turn_m(h, q):
+            for g in range(GM):
+                banks[("m", h, q, g)] = turn(
+                    lambda j, u: word_columns(m_in[(h, 2 * q + j)], m_words.get((h, 2 * q + j)), g, u)
+                )
+
+        def scale_m(h, q):
+            for g in range(GM):
+                nc.vector.tensor_tensor(
+                    out=m_g[:, h, g, q * 1024 : (q + 1) * 1024].rearrange("p (c u e) -> p c u e", u=2, e=2),
+                    in0=banks[("m", h, q, g)][:].bitcast(BF16).rearrange("p (u c e) -> p c u e", u=2, e=2),
+                    in1=m_fac[:, g, :].rearrange("p (u e) -> p u e", e=2).unsqueeze(1).to_broadcast([128, 256, 2, 2]),
+                    op=ALU.mult,
+                )
+            for g in range(GM):
+                quantize(m_g, m_c, m_s, h, q, g)
+
+        def write_products(h, q):
             bank = psum.tile([128, 512], F32, name="bank")
             for x in range(8):
+                lo = q * 1024 + x * 128
                 for g in range(GZ):
-                    lo = q * 1024 + x * 128
                     nc.tensor.matmul(
                         bank[:, 4 * x : 4 * x + 4],
                         lhsT=z_g[:, h, g, lo : lo + 128],
@@ -177,138 +222,87 @@ def tile_legendrememoryunitstep_w8_kernel(
                         start=(g == 0),
                         stop=(g == GZ - 1),
                     )
-            banks[("u", h, q)] = bank
-
-        def pick_products(h, q):
-            prod = small.tile([128, 8, 4], F32, name="prod")
+            kept = small.tile([128, 8, 4], F32, name="kept")
             nc.vector.tensor_tensor(
-                out=prod[:],
-                in0=banks[("u", h, q)][:, 0:32].rearrange("p (x t) -> p x t", t=4),
+                out=kept[:],
+                in0=bank[:, 0:32].rearrange("p (x t) -> p x t", t=4),
                 in1=same_t[:].unsqueeze(1).to_broadcast([128, 8, 4]),
                 op=ALU.mult,
             )
-            banks[("prod", h, q)] = prod
+            banks[("kept", h, q)] = kept
 
-        def gather_scalar(h, q):
+        def sum_products(h, q):
             bank = psum.tile([128, 512], F32, name="bank")
             nc.tensor.matmul(
                 bank[:, 0:32],
-                lhsT=gather[:].rearrange("p b j -> p (b j)"),
-                rhs=banks[("prod", h, q)][:].rearrange("p x t -> p (x t)"),
+                lhsT=gather[:].rearrange("p b i -> p (b i)"),
+                rhs=banks[("kept", h, q)][:].rearrange("p x t -> p (x t)"),
                 start=True,
                 stop=True,
             )
-            banks[("w", h, q)] = bank
-
-        def take_scalar(h, q):
             part = small.tile([128, 2, 16], F32, name="part")
             nc.vector.tensor_tensor(
                 out=part[:],
-                in0=banks[("w", h, q)][:, 0:32].rearrange("p (j x) -> p j x", j=2),
-                in1=quad_t[:].rearrange("p b t -> p (b t)").unsqueeze(1).to_broadcast([128, 2, 16]),
+                in0=bank[:, 0:32].rearrange("p (j x) -> p j x", j=2),
+                in1=block_t[:].rearrange("p b t -> p (b t)").unsqueeze(1).to_broadcast([128, 2, 16]),
                 op=ALU.mult,
             )
             nc.vector.tensor_reduce(out=u_col[:, h, 2 * q : 2 * q + 2], in_=part[:], axis=AX.X, op=ALU.add)
 
-        def cast_m(h, r, engine="s"):
-            mt = mrows.tile([128, 1024], BF16, name="mt")
-            copy = nc.vector.tensor_copy if engine == "v" else nc.scalar.copy
-            copy(out=mt[:], in_=m_raw[:, h, r * 1024 : (r + 1) * 1024].bitcast(FP8))
-            m_bf[(h, r)] = mt
-
-        def pre_m(h, r, engine="v"):
-            mp = mwords.tile([128, 512], F32, name="mp")
-            copy = nc.vector.tensor_copy if engine == "v" else nc.scalar.copy
-            copy(
-                out=mp[:].rearrange("p (u c) -> p u c", u=2),
-                in_=m_bf[(h, r)][:].bitcast(F32).rearrange("p (c u) -> p u c", u=2),
-            )
-            m_pre[(h, r)] = mp
-
-        def turn_m(h, q, g):
-            bank = psum.tile([128, 512], F32, name="bank")
-            for j in range(2):
-                r = 2 * q + j
-                for u in range(2):
-                    if (h, r) in m_pre:
-                        words = m_pre[(h, r)][:, 256 * u + 128 * g : 256 * u + 128 * (g + 1)]
-                    else:
-                        words = m_bf[(h, r)][:].bitcast(F32)[:, 256 * g + u : 256 * (g + 1) : 2]
-                    nc.tensor.transpose(
-                        bank[:, u * 256 + j * 128 : u * 256 + (j + 1) * 128],
-                        words,
-                        ident[:],
-                    )
-            banks[("m", h, q, g)] = bank
-
-        def take_m(h, q, g):
-            bank = banks[("m", h, q, g)]
-            nc.vector.tensor_tensor(
-                out=m_g[:, h, g, q * 1024 : (q + 1) * 1024].rearrange("p (c u e) -> p c u e", u=2, e=2),
-                in0=bank[:].bitcast(BF16).rearrange("p (u c e) -> p c u e", u=2, e=2),
-                in1=m_fac[:, g, :].rearrange("p (u e) -> p u e", e=2).unsqueeze(1).to_broadcast([128, 256, 2, 2]),
-                op=ALU.mult,
-            )
-
-        def memory(h, r, c):
-            bank = psum.tile([128, 512], F32, name="bank")
+        def memory(h, r):
+            nt = nrows.tile([128, P], BF16, name="nt")
+            n_in[(h, r)] = nt
             rows = slice(r * 128, (r + 1) * 128)
-            cols = slice(c * 512, (c + 1) * 512)
+            for c in range(GM):
+                cols = slice(c * 512, (c + 1) * 512)
+                bank = psum.tile([128, 512], F32, name="bank")
+                for g in range(GM):
+                    nc.tensor.matmul_mx(
+                        out=bank[:],
+                        lhsT=m_c[:, h, g, rows].bitcast(FP8X4),
+                        lhsT_scale=m_s[:, h, g, rows],
+                        rhs=at_c[:, g, cols].bitcast(FP8X4),
+                        rhs_scale=at_s[4 * g : 128, cols],
+                        start=(g == 0),
+                        stop=(g == GM - 1),
+                    )
+                for u in range(2):
+                    lo = c * 512 + u * 256
+                    nc.vector.scalar_tensor_tensor(
+                        out=nt[:, lo : lo + 256].rearrange("p (x e) -> p x e", e=2),
+                        in0=b_all[:, c, u * 256 : (u + 1) * 256].rearrange("p (x e) -> p x e", e=2),
+                        scalar=u_col[:, h, r : r + 1],
+                        in1=bank[:].rearrange("p (x u e) -> p u x e", u=2, e=2)[:, u],
+                        op0=ALU.mult,
+                        op1=ALU.add,
+                    )
+
+        def turn_n(h, q):
             for g in range(GM):
-                nc.tensor.matmul_mx(
-                    out=bank[:],
-                    lhsT=m_c[:, h, g, rows].bitcast(FP8X4),
-                    lhsT_scale=m_s[:, h, g, rows],
-                    rhs=at_c[:, g, cols].bitcast(FP8X4),
-                    rhs_scale=at_s[4 * g : 128, cols],
-                    start=(g == 0),
-                    stop=(g == GM - 1),
-                )
-            banks[("n", h, r, c)] = bank
-
-        def take_memory(h, r, c):
-            if (h, r) not in n_rows:
-                nr = nrows.tile([128, 1024], BF16, name="nr")
-                n_rows[(h, r)] = nr
-            for u in range(2):
-                lo = c * 512 + u * 256
-                nc.vector.scalar_tensor_tensor(
-                    out=n_rows[(h, r)][:, lo : lo + 256].rearrange("p (x e) -> p x e", e=2),
-                    in0=b_bc[:, c, u * 256 : (u + 1) * 256].rearrange("p (x e) -> p x e", e=2),
-                    scalar=u_col[:, h, r : r + 1],
-                    in1=banks[("n", h, r, c)][:].rearrange("p (x u e) -> p u x e", u=2, e=2)[:, u],
-                    op0=ALU.mult,
-                    op1=ALU.add,
+                banks[("n", h, q, g)] = turn(
+                    lambda j, u: n_in[(h, 2 * q + j)][:].bitcast(F32)[:, 256 * g + 128 * u : 256 * g + 128 * (u + 1)]
                 )
 
-        def turn_n(h, q, g):
-            bank = psum.tile([128, 512], F32, name="bank")
-            for j in range(2):
-                words = n_rows[(h, 2 * q + j)][:].bitcast(F32)
-                for u in range(2):
-                    nc.tensor.transpose(
-                        bank[:, u * 256 + j * 128 : u * 256 + (j + 1) * 128],
-                        words[:, g * 256 + u * 128 : g * 256 + (u + 1) * 128],
-                        ident[:],
-                    )
-            banks[("t", h, q, g)] = bank
+        def take_n(h, q, copy):
+            for g in range(GM):
+                take_words(n_g[:, h, g, q * 1024 : (q + 1) * 1024], banks[("n", h, q, g)], copy)
 
-        def take_n(h, q, g, engine="s"):
-            copy = nc.vector.tensor_copy if engine == "v" else nc.scalar.copy
-            copy(
-                out=n_g[:, h, g, q * 1024 : (q + 1) * 1024].bitcast(F32),
-                in_=banks[("t", h, q, g)][:].rearrange("p (u c) -> p c u", u=2),
-            )
+        def quantize_n(h, q):
+            for g in range(GM):
+                quantize(n_g, n_c, n_s, h, q, g)
 
-        def finish_z(h, r, c):
-            bank = psum.tile([128, 512], F32, name="bank")
-            banks[("f", h, r, c)] = bank
+        def out_columns(h, r, c):
+            width = 256 if (h, r) == (1, 3) else 512
+            return width, slice(c * width, (c + 1) * width)
+
+        def start_out(h, r, c):
+            width, cols = out_columns(h, r, c)
             rows = slice(r * 128, (r + 1) * 128)
-            w = 256 if (h, r) == (1, 3) else 512
-            cols = slice(c * w, (c + 1) * w)
+            bank = psum.tile([128, 512], F32, name="bank")
+            banks[("out", h, r, c)] = bank
             for g in range(GZ):
                 nc.tensor.matmul_mx(
-                    out=bank[:, 0:w],
+                    out=bank[:, 0:width],
                     lhsT=z_c[:, h, g, rows].bitcast(FP8X4),
                     lhsT_scale=z_s[:, h, g, rows],
                     rhs=wz_c[:, g, cols].bitcast(FP8X4),
@@ -317,14 +311,13 @@ def tile_legendrememoryunitstep_w8_kernel(
                     stop=False,
                 )
 
-        def finish_n(h, r, c):
-            bank = banks[("f", h, r, c)]
+        def end_out(h, r, c):
+            width, cols = out_columns(h, r, c)
             rows = slice(r * 128, (r + 1) * 128)
-            w = 256 if (h, r) == (1, 3) else 512
-            cols = slice(c * w, (c + 1) * w)
+            bank = banks[("out", h, r, c)]
             for g in range(GM):
                 nc.tensor.matmul_mx(
-                    out=bank[:, 0:w],
+                    out=bank[:, 0:width],
                     lhsT=n_c[:, h, g, rows].bitcast(FP8X4),
                     lhsT_scale=n_s[:, h, g, rows],
                     rhs=wm_c[:, g, cols].bitcast(FP8X4),
@@ -332,280 +325,148 @@ def tile_legendrememoryunitstep_w8_kernel(
                     start=False,
                     stop=(g == GM - 1),
                 )
-
-        def squash(h, r, c):
             res = results.tile([128, 512], F32, name="res")
-            w = 256 if (h, r) == (1, 3) else 512
-            nc.scalar.activation(out=res[:, 0:w], in_=banks[("f", h, r, c)][:, 0:w], func=ACT.Tanh)
-            banks[("r", h, r, c)] = res
+            nc.scalar.activation(out=res[:, 0:width], in_=bank[:, 0:width], func=ACT.Tanh)
+            nc.sync.dma_start(out=out_rows[h][:, r, cols], in_=res[:, 0:width])
 
-        def store(h, r, c):
-            w = 256 if (h, r) == (1, 3) else 512
-            nc.sync.dma_start(out=out_rows[h][:, r, c * w : (c + 1) * w], in_=banks[("r", h, r, c)][:, 0:w])
-
-        make_identity(nc, ident[:])
-        nc.vector.memset(warm[:], 0.0)
+        nc.vector.memset(table[:], 0.0)
         nc.vector.memset(ones[:], 1.0)
         nc.vector.memset(b_row[:], 0.0)
-        nc.vector.memset(at_s[:].bitcast(I32), 0)
-        nc.vector.memset(wz_s[:].bitcast(I32), 0)
-        nc.vector.memset(wm_s[:].bitcast(I32), 0)
-        nc.scalar.activation(out=warm[:], in_=warm[:], func=ACT.Tanh)
-        warm_up()
-        make_masks()
-        warm_up()
-        warm_up()
-        load_m(0, 1)
-        cast_m(0, 3, "v")
-        cast_m(0, 2, "s")
-        turn_m(0, 1, 0)
-        turn_m(0, 1, 1)
-        load_m(0, 0)
-        cast_m(0, 0, "v")
-        warm_up()
-        load_m(1, 0)
-        cast_m(1, 0, "s")
-        cast_m(1, 1, "s")
-        warm_up()
-        cast_m(0, 1, "v")
-        turn_m(0, 0, 0)
-        load_small(m_fac, m_scale.rearrange("o (g p t) -> p (o g) t", p=128, t=4))
-        take_m(0, 1, 0)
-        take_m(0, 1, 1)
-        quant(m_g, m_c, m_s, 0, 1, 0)
-        take_m(0, 0, 0)
-        load_z(0, 0)
-        load_b()
-        spread_b(1)
-        take_b(1, "v")
-        pre_m(1, 0, "s")
-        load_z(1, 3)
-        pre_z(1, 3, "s")
-        load_z(1, 1)
-        pre_z(1, 1, "s")
-        load_z(0, 1)
-        turn_z(0, 0, 2, direct=True)
-        take_z(0, 0, 2, "s")
-        quant(z_g, z_c, z_s, 0, 0, 2)
-        turn_z(0, 0, 1, direct=True)
-        turn_z(0, 0, 0, direct=True)
-        take_z(0, 0, 0, "s")
-        quant(z_g, z_c, z_s, 0, 0, 0)
-        take_z(0, 0, 1, "s")
-        pre_m(1, 1, "v")
-        turn_m(0, 0, 1)
-        take_m(0, 0, 1)
+        for planes in (at_s, wz_s, wm_s):
+            nc.vector.memset(planes[:].bitcast(I32), 0)
+        make_identity(nc, ident[:])
+        nc.scalar.activation(out=table[:], in_=table[:], func=ACT.Tanh)
+
+        load_m(0, 0, 1)
+        load_m(0, 1, 2)
         load_z(0, 3)
-        warm_up()
-        quant(m_g, m_c, m_s, 0, 1, 1)
+        load_m(0, 2, 4)
+        load_small(m_fac[:], m_scale.rearrange("o (g p t) -> p (o g) t", p=128, t=4))
         load_z(0, 2)
-        turn_z(0, 1, 1, direct=True)
-        take_z(0, 1, 1, "s")
-        quant(z_g, z_c, z_s, 0, 1, 1)
-        turn_z(0, 1, 2, direct=True)
-        take_z(0, 1, 2, "s")
-        quant(z_g, z_c, z_s, 0, 1, 2)
-        turn_z(0, 1, 0, direct=True)
-        turn_m(1, 0, 0)
-        take_m(1, 0, 0)
-        load_small(ez_col, ez.rearrange("(g p t) -> p g t", p=128, t=4))
-        write_scalar(0, 0)
-        pick_products(0, 0)
-        load_words(at_c, at_words, 0)
-        take_z(0, 1, 0, "s")
-        write_scalar(0, 1)
-        pick_products(0, 1)
-        quant(m_g, m_c, m_s, 0, 0, 1)
-        load_words(at_c, at_words, 1)
-        quant(m_g, m_c, m_s, 0, 0, 0)
         load_z(1, 2)
-        pre_z(1, 2, "s")
-        turn_z(1, 1, 0)
-        take_z(1, 1, 0, "v")
-        spread_b(0)
-        take_b(0, "v")
+        load_z(1, 3)
+        load_z(0, 1, 0, 512)
+        load_z(0, 0, 512, K)
+        load_small(b_row[0:1, :], bvec.rearrange("(o n) -> o n", o=1))
+        load_z(0, 1, 512, K)
+        load_z(0, 0, 0, 512)
         load_z(1, 0)
-        pre_z(1, 0, "s")
-        turn_z(1, 0, 2)
-        turn_z(1, 0, 1)
-        take_z(1, 0, 2, "s")
-        take_z(1, 0, 1, "s")
-        quant(z_g, z_c, z_s, 1, 0, 2)
-        turn_z(1, 0, 0)
-        take_z(1, 0, 0, "s")
-        warm_up()
-        quant(z_g, z_c, z_s, 1, 1, 0)
-        gather_scalar(0, 1)
-        take_scalar(0, 1)
-        gather_scalar(0, 0)
-        take_scalar(0, 0)
+        load_z(1, 1)
+        load_small(ez_col[:], ez.rearrange("(g p t) -> p g t", p=128, t=4))
+        load_words(at_c, at_words, 1)
         load_words(wz_c, wz_words, 0)
-        turn_m(1, 0, 1)
-        take_m(1, 0, 1)
-        turn_z(1, 1, 2)
-        take_z(1, 1, 2, "s")
-        load_m(1, 1)
-        cast_m(1, 3, "s")
-        cast_m(1, 2, "s")
-        pre_m(1, 3, "s")
-        pre_m(1, 2, "s")
-        load_scales(wm_s, wm_scales, GM)
-        load_words(wz_c, wz_words, 2)
-        write_scalar(1, 0)
-        pick_products(1, 0)
+        load_m(1, 2, 4)
         load_scales(at_s, at_scales, GM)
-        memory(0, 0, 0)
-        memory(0, 1, 0)
-        memory(0, 1, 1)
-        take_memory(0, 0, 0)
-        take_memory(0, 1, 0)
-        memory(0, 2, 0)
-        memory(0, 2, 1)
-        take_memory(0, 1, 1)
-        take_memory(0, 2, 0)
-        take_memory(0, 2, 1)
-        memory(0, 0, 1)
-        take_memory(0, 0, 1)
-        memory(0, 3, 1)
-        take_memory(0, 3, 1)
-        turn_z(1, 1, 1)
-        take_z(1, 1, 1, "s")
-        memory(0, 3, 0)
-        take_memory(0, 3, 0)
+        load_words(at_c, at_words, 0)
+        load_m(1, 0, 2)
         load_words(wm_c, wm_words, 0)
-        gather_scalar(1, 0)
-        take_scalar(1, 0)
-        load_words(wz_c, wz_words, 1)
-        turn_n(0, 0, 0)
-        take_n(0, 0, 0, "s")
-        write_scalar(1, 1)
-        pick_products(1, 1)
-        warm_up()
-        quant(z_g, z_c, z_s, 0, 0, 1)
-        turn_n(0, 0, 1)
-        quant(n_g, n_c, n_s, 0, 0, 0)
-        turn_n(0, 1, 1)
-        take_n(0, 1, 1, "s")
-        quant(n_g, n_c, n_s, 0, 1, 1)
-        turn_m(1, 1, 1)
-        take_m(1, 1, 1)
-        take_n(0, 0, 1, "s")
-        quant(n_g, n_c, n_s, 0, 0, 1)
-        quant(m_g, m_c, m_s, 1, 0, 1)
-        quant(z_g, z_c, z_s, 1, 0, 0)
-        turn_n(0, 1, 0)
-        take_n(0, 1, 0, "s")
-        quant(n_g, n_c, n_s, 0, 1, 0)
-        quant(z_g, z_c, z_s, 0, 1, 0)
-        load_words(wm_c, wm_words, 1)
-        turn_m(1, 1, 0)
-        take_m(1, 1, 0)
-        quant(m_g, m_c, m_s, 1, 1, 0)
-        quant(z_g, z_c, z_s, 1, 1, 2)
-        gather_scalar(1, 1)
-        take_scalar(1, 1)
         load_scales(wz_s, wz_scales, GZ)
-        finish_z(0, 0, 1)
-        finish_z(0, 0, 0)
-        finish_z(0, 1, 1)
-        finish_n(0, 1, 1)
-        finish_z(0, 1, 0)
-        finish_n(0, 1, 0)
-        squash(0, 1, 0)
-        store(0, 1, 0)
-        squash(0, 1, 1)
-        store(0, 1, 1)
-        finish_z(0, 3, 1)
-        finish_n(0, 3, 1)
-        squash(0, 3, 1)
-        store(0, 3, 1)
-        finish_n(0, 0, 0)
-        squash(0, 0, 0)
-        store(0, 0, 0)
-        finish_n(0, 0, 1)
-        squash(0, 0, 1)
-        store(0, 0, 1)
-        quant(m_g, m_c, m_s, 1, 1, 1)
-        memory(1, 3, 0)
-        take_memory(1, 3, 0)
-        memory(1, 2, 0)
-        take_memory(1, 2, 0)
-        memory(1, 2, 1)
-        take_memory(1, 2, 1)
-        memory(1, 3, 1)
-        take_memory(1, 3, 1)
-        finish_z(0, 2, 1)
-        finish_n(0, 2, 1)
-        squash(0, 2, 1)
-        store(0, 2, 1)
-        finish_z(0, 2, 0)
-        finish_n(0, 2, 0)
-        squash(0, 2, 0)
-        store(0, 2, 0)
-        quant(m_g, m_c, m_s, 1, 0, 0)
-        memory(1, 1, 1)
-        take_memory(1, 1, 1)
-        memory(1, 0, 1)
-        take_memory(1, 0, 1)
-        memory(1, 0, 0)
-        take_memory(1, 0, 0)
-        memory(1, 1, 0)
-        take_memory(1, 1, 0)
-        turn_n(1, 1, 0)
-        take_n(1, 1, 0, "s")
-        quant(n_g, n_c, n_s, 1, 1, 0)
-        finish_z(0, 3, 0)
-        finish_n(0, 3, 0)
-        squash(0, 3, 0)
-        store(0, 3, 0)
-        turn_n(1, 1, 1)
-        turn_n(1, 0, 0)
-        take_n(1, 0, 0, "s")
-        turn_n(1, 0, 1)
-        quant(z_g, z_c, z_s, 1, 0, 1)
-        finish_z(1, 1, 0)
-        finish_z(1, 0, 0)
-        finish_z(1, 1, 1)
-        finish_z(1, 0, 1)
-        take_n(1, 1, 1, "v")
-        quant(n_g, n_c, n_s, 1, 1, 1)
-        quant(n_g, n_c, n_s, 1, 0, 0)
-        take_n(1, 0, 1, "s")
-        quant(n_g, n_c, n_s, 1, 0, 1)
-        finish_n(1, 0, 1)
-        squash(1, 0, 1)
-        finish_n(1, 0, 0)
-        finish_n(1, 1, 1)
-        squash(1, 0, 0)
-        store(1, 0, 0)
-        store(1, 0, 1)
-        squash(1, 1, 1)
-        store(1, 1, 1)
-        finish_n(1, 1, 0)
-        squash(1, 1, 0)
-        store(1, 1, 0)
-        quant(z_g, z_c, z_s, 1, 1, 1)
-        finish_z(1, 2, 0)
-        finish_z(1, 2, 1)
-        finish_n(1, 2, 0)
-        finish_z(1, 3, 1)
-        finish_n(1, 3, 1)
-        finish_n(1, 2, 1)
-        squash(1, 3, 1)
-        store(1, 3, 1)
-        squash(1, 2, 1)
-        store(1, 2, 1)
-        finish_z(1, 3, 3)
-        squash(1, 2, 0)
-        store(1, 2, 0)
-        finish_n(1, 3, 3)
-        squash(1, 3, 3)
-        store(1, 3, 3)
-        finish_z(1, 3, 0)
-        finish_n(1, 3, 0)
-        squash(1, 3, 0)
-        store(1, 3, 0)
-        finish_z(1, 3, 2)
-        finish_n(1, 3, 2)
-        squash(1, 3, 2)
-        store(1, 3, 2)
+        load_words(wz_c, wz_words, 2)
+        load_words(wz_c, wz_words, 1)
+        load_words(wm_c, wm_words, 1)
+        load_scales(wm_s, wm_scales, GM)
+
+        for dummy in range(6):
+            keep_busy()
+        make_masks()
+        widen_m(0, 0, on_vector)
+        turn_m(0, 0)
+        widen_m(0, 1, on_vector)
+        scale_m(0, 0)
+        for dummy in range(2):
+            keep_busy()
+        order_m(0, 1, on_scalar)
+        turn_z(0, 1)
+        keep_busy()
+        order_z(1, 1, on_scalar)
+        turn_m(0, 1)
+        scale_m(0, 1)
+        take_z(0, 1, on_scalar)
+        quantize_z(0, 1)
+        turn_z(1, 1)
+        take_z(1, 1, on_scalar)
+        keep_busy()
+        turn_z(0, 0)
+        take_z(0, 0, on_scalar)
+        keep_busy()
+        order_z(1, 0, on_vector)
+        quantize_z(0, 0)
+        keep_busy()
+        write_products(0, 1)
+        write_products(1, 1)
+        spread_b()
+        take_b(on_scalar)
+        write_products(0, 0)
+        widen_m(1, 1, on_vector)
+        turn_z(1, 0)
+        sum_products(0, 0)
+        take_z(1, 0, on_scalar)
+        sum_products(0, 1)
+        memory(0, 0)
+        memory(0, 3)
+        memory(0, 1)
+        write_products(1, 0)
+        widen_m(1, 0, on_scalar)
+        order_m(1, 0, on_scalar)
+        memory(0, 2)
+        turn_n(0, 0)
+        sum_products(1, 0)
+        sum_products(1, 1)
+        order_m(1, 1, on_scalar)
+        turn_m(1, 1)
+        scale_m(1, 1)
+        take_n(0, 0, on_scalar)
+        quantize_n(0, 0)
+        turn_n(0, 1)
+        take_n(0, 1, on_scalar)
+        quantize_n(0, 1)
+        turn_m(1, 0)
+        start_out(0, 0, 0)
+        start_out(0, 2, 0)
+        start_out(0, 1, 1)
+        start_out(0, 0, 1)
+        start_out(0, 2, 1)
+        start_out(0, 3, 1)
+        end_out(0, 0, 0)
+        end_out(0, 2, 0)
+        end_out(0, 3, 1)
+        end_out(0, 2, 1)
+        end_out(0, 1, 1)
+        end_out(0, 0, 1)
+        scale_m(1, 0)
+        memory(1, 1)
+        memory(1, 0)
+        memory(1, 2)
+        memory(1, 3)
+        start_out(0, 1, 0)
+        end_out(0, 1, 0)
+        start_out(0, 3, 0)
+        end_out(0, 3, 0)
+        turn_n(1, 0)
+        turn_n(1, 1)
+        take_n(1, 1, on_scalar)
+        quantize_z(1, 0)
+        start_out(1, 1, 1)
+        start_out(1, 0, 1)
+        start_out(1, 0, 0)
+        start_out(1, 1, 0)
+        take_n(1, 0, on_vector)
+        quantize_n(1, 0)
+        end_out(1, 0, 1)
+        end_out(1, 1, 0)
+        end_out(1, 1, 1)
+        end_out(1, 0, 0)
+        quantize_n(1, 1)
+        quantize_z(1, 1)
+        start_out(1, 2, 0)
+        start_out(1, 3, 1)
+        start_out(1, 3, 3)
+        end_out(1, 3, 3)
+        end_out(1, 2, 0)
+        start_out(1, 2, 1)
+        end_out(1, 2, 1)
+        end_out(1, 3, 1)
+        start_out(1, 3, 2)
+        end_out(1, 3, 2)
+        start_out(1, 3, 0)
+        end_out(1, 3, 0)

from contextlib import ExitStack

import concourse.mybir as mybir
from concourse.masks import make_identity

N, K, P, H = 1024, 1536, 1024, 1024
FLOPS = 2 * N * P * P + 2 * N * (K + P) * H

F32 = mybir.dt.float32
BF16 = mybir.dt.bfloat16
I32 = mybir.dt.int32
U8 = mybir.dt.uint8
FP8 = mybir.dt.float8_e4m3fn
FP8X4 = mybir.dt.float8_e4m3fn_x4
ACT = mybir.ActivationFunctionType
ALU = mybir.AluOpType
AX = mybir.AxisListType

GZ = K // 512
GM = P // 512


def tile_legendrememoryunitstep_w8_kernel(
    tc, z, m_bytes, m_scale, ez, at_words, at_scales, bvec, wz_words, wz_scales, wm_words, wm_scales, out
):
    nc = tc.nc
    on_vector = nc.vector.tensor_copy
    on_scalar = nc.scalar.copy

    with ExitStack() as ctx:
        keep = ctx.enter_context(tc.tile_pool(name="keep", bufs=1))
        zrows = ctx.enter_context(tc.tile_pool(name="zrows", bufs=8))
        words_pool = ctx.enter_context(tc.tile_pool(name="words", bufs=4))
        mrows = ctx.enter_context(tc.tile_pool(name="mrows", bufs=4))
        nrows = ctx.enter_context(tc.tile_pool(name="nrows", bufs=8))
        small = ctx.enter_context(tc.tile_pool(name="small", bufs=4))
        results = ctx.enter_context(tc.tile_pool(name="results", bufs=8))
        psum = ctx.enter_context(tc.psum_pool(name="psum", bufs=8))
        ctx.enter_context(tc.manual_schedule())

        z_rows = z.rearrange("(h p r) k -> h p r k", h=2, p=128)
        m_rows = m_bytes.rearrange("(h p r) k -> h p (r k)", h=2, p=128)
        out_rows = out.rearrange("(h p r) c -> h p r c", h=2, p=128)

        ident = keep.tile([128, 128], F32, name="ident")
        ones = keep.tile([128, 512], BF16, name="ones")
        table = keep.tile([128, 1], F32, name="table")
        ez_col = keep.tile([128, GZ, 4], BF16, name="ez_col")
        m_fac = keep.tile([128, GM, 4], F32, name="m_fac")
        m_raw = keep.tile([128, 2, 4 * P], U8, name="m_raw")
        b_row = keep.tile([128, P], BF16, name="b_row")
        b_all = keep.tile([128, GM, 512], BF16, name="b_all")

        same_t = keep.tile([128, 4], F32, name="same_t")
        row_of = keep.tile([128, 32], F32, name="row_of")
        gather = keep.tile([128, 4, 32], F32, name="gather")
        block_of = keep.tile([128, 4], F32, name="block_of")
        block_t = keep.tile([128, 4, 4], F32, name="block_t")
        u_col = keep.tile([128, 2, 4], F32, name="u_col")

        at_c = keep.tile([128, GM, P], I32, name="at_c", align_bytes=64)
        at_s = keep.tile([128, P], U8, name="at_s", align_bytes=64)
        wz_c = keep.tile([128, GZ, H], I32, name="wz_c", align_bytes=64)
        wz_s = keep.tile([128, H], U8, name="wz_s", align_bytes=64)
        wm_c = keep.tile([128, GM, H], I32, name="wm_c", align_bytes=64)
        wm_s = keep.tile([128, H], U8, name="wm_s", align_bytes=64)
        z_g = keep.tile([128, 2, GZ, 2048], BF16, name="z_g", align_bytes=64)
        z_c = keep.tile([128, 2, GZ, 512], I32, name="z_c", align_bytes=64)
        z_s = keep.tile([128, 2, GZ, 512], U8, name="z_s", align_bytes=64)
        m_g = keep.tile([128, 2, GM, 2048], BF16, name="m_g", align_bytes=64)
        m_c = keep.tile([128, 2, GM, 512], I32, name="m_c", align_bytes=64)
        m_s = keep.tile([128, 2, GM, 512], U8, name="m_s", align_bytes=64)
        n_g = keep.tile([128, 2, GM, 2048], BF16, name="n_g", align_bytes=64)
        n_c = keep.tile([128, 2, GM, 512], I32, name="n_c", align_bytes=64)
        n_s = keep.tile([128, 2, GM, 512], U8, name="n_s", align_bytes=64)

        z_in, z_words, m_in, m_words, n_in, banks = {}, {}, {}, {}, {}, {}

        def load_z(h, r, lo=0, hi=K):
            if (h, r) not in z_in:
                zt = zrows.tile([128, K], BF16, name="zt")
                z_in[(h, r)] = zt
            nc.sync.dma_start(out=z_in[(h, r)][:, lo:hi], in_=z_rows[h][:, r, lo:hi])

        def load_m(h, first, end):
            cols = slice(first * P, end * P)
            nc.sync.dma_start(out=m_raw[:, h, cols], in_=m_rows[h][:, cols])

        def load_words(codes, words, g):
            nc.sync.dma_start(out=codes[:, g, :], in_=words[g].rearrange("p n t -> p (n t)").bitcast(I32))

        def load_scales(planes, scales, passes):
            for quadrant in range(4):
                nc.sync.dma_start(
                    out=planes[32 * quadrant : 32 * quadrant + 4 * passes, :].bitcast(I32),
                    in_=scales[:, 4 * quadrant : 4 * quadrant + 4, :].bitcast(I32),
                )

        def load_small(dst, src):
            nc.sync.dma_start(out=dst, in_=src)

        def make_masks():
            for mask, view in (
                (same_t, ident[:].rearrange("p (j t) -> p t j", t=4)),
                (row_of, ident[:].rearrange("p (j t) -> p j t", t=4)),
                (block_of, ident[:].rearrange("p (b i) -> p b i", b=4)),
            ):
                nc.vector.tensor_reduce(out=mask[:], in_=view, axis=AX.X, op=ALU.add)
            nc.vector.tensor_copy(out=gather[:], in_=row_of[:].unsqueeze(1).to_broadcast([128, 4, 32]))
            nc.vector.tensor_copy(out=block_t[:], in_=block_of[:].unsqueeze(2).to_broadcast([128, 4, 4]))

        def keep_busy():
            bank = psum.tile([128, 512], F32, name="bank")
            nc.tensor.matmul(bank[:], lhsT=ones[:, 0:128], rhs=ones[:], start=True, stop=True)

        def spread_b():
            for c in range(GM):
                bank = psum.tile([128, 512], F32, name="bank")
                nc.tensor.matmul(
                    bank[:], lhsT=ones[:, 0:128], rhs=b_row[:, c * 512 : (c + 1) * 512], start=True, stop=True
                )
                banks[("b", c)] = bank

        def take_b(copy):
            for c in range(GM):
                copy(
                    out=b_all[:, c, :].rearrange("p (u x e) -> p u x e", u=2, e=2),
                    in_=banks[("b", c)][:].rearrange("p (x u e) -> p u x e", u=2, e=2),
                )

        def pair(q):
            return (2 * q, 2 * q + 1)

        def order_words(rows, copy):
            src = rows[:].bitcast(F32)
            ordered = words_pool.tile([128, src.shape[1]], F32, name="ordered%d" % src.shape[1])
            copy(
                out=ordered[:].rearrange("p (u c) -> p u c", u=2),
                in_=src.rearrange("p (c u) -> p u c", u=2),
            )
            return ordered

        def word_columns(rows, ordered, g, u):
            if ordered is None:
                return rows[:].bitcast(F32)[:, 256 * g + u : 256 * (g + 1) : 2]
            lo = u * (ordered.shape[1] // 2) + 128 * g
            return ordered[:, lo : lo + 128]

        def turn(columns):
            bank = psum.tile([128, 512], F32, name="bank")
            for j in range(2):
                for u in range(2):
                    lo = 256 * u + 128 * j
                    nc.tensor.transpose(bank[:, lo : lo + 128], columns(j, u), ident[:])
            return bank

        def take_words(grouped, bank, copy):
            copy(out=grouped.bitcast(F32), in_=bank[:].rearrange("p (u c) -> p c u", u=2))

        def quantize(grouped, codes, scales, h, q, g):
            cols = slice(q * 256, (q + 1) * 256)
            nc.vector.quantize_mx(
                out=codes[:, h, g, cols].bitcast(FP8X4),
                scales=scales[:, h, g, cols],
                in_=grouped[:, h, g, q * 1024 : (q + 1) * 1024],
            )

        def order_z(h, q, copy):
            for r in pair(q):
                z_words[(h, r)] = order_words(z_in[(h, r)], copy)

        def turn_z(h, q):
            for g in range(GZ):
                banks[("z", h, q, g)] = turn(
                    lambda j, u: word_columns(z_in[(h, 2 * q + j)], z_words.get((h, 2 * q + j)), g, u)
                )

        def take_z(h, q, copy):
            for g in range(GZ):
                take_words(z_g[:, h, g, q * 1024 : (q + 1) * 1024], banks[("z", h, q, g)], copy)

        def quantize_z(h, q):
            for g in range(GZ):
                quantize(z_g, z_c, z_s, h, q, g)

        def widen_m(h, q, copy):
            for r in pair(q):
                mt = mrows.tile([128, P], BF16, name="mt")
                copy(out=mt[:], in_=m_raw[:, h, r * P : (r + 1) * P].bitcast(FP8))
                m_in[(h, r)] = mt

        def order_m(h, q, copy):
            for r in pair(q):
                m_words[(h, r)] = order_words(m_in[(h, r)], copy)

        def turn_m(h, q):
            for g in range(GM):
                banks[("m", h, q, g)] = turn(
                    lambda j, u: word_columns(m_in[(h, 2 * q + j)], m_words.get((h, 2 * q + j)), g, u)
                )

        def scale_m(h, q):
            for g in range(GM):
                nc.vector.tensor_tensor(
                    out=m_g[:, h, g, q * 1024 : (q + 1) * 1024].rearrange("p (c u e) -> p c u e", u=2, e=2),
                    in0=banks[("m", h, q, g)][:].bitcast(BF16).rearrange("p (u c e) -> p c u e", u=2, e=2),
                    in1=m_fac[:, g, :].rearrange("p (u e) -> p u e", e=2).unsqueeze(1).to_broadcast([128, 256, 2, 2]),
                    op=ALU.mult,
                )
            for g in range(GM):
                quantize(m_g, m_c, m_s, h, q, g)

        def write_products(h, q):
            bank = psum.tile([128, 512], F32, name="bank")
            for x in range(8):
                lo = q * 1024 + x * 128
                for g in range(GZ):
                    nc.tensor.matmul(
                        bank[:, 4 * x : 4 * x + 4],
                        lhsT=z_g[:, h, g, lo : lo + 128],
                        rhs=ez_col[:, g, :],
                        start=(g == 0),
                        stop=(g == GZ - 1),
                    )
            kept = small.tile([128, 8, 4], F32, name="kept")
            nc.vector.tensor_tensor(
                out=kept[:],
                in0=bank[:, 0:32].rearrange("p (x t) -> p x t", t=4),
                in1=same_t[:].unsqueeze(1).to_broadcast([128, 8, 4]),
                op=ALU.mult,
            )
            banks[("kept", h, q)] = kept

        def sum_products(h, q):
            bank = psum.tile([128, 512], F32, name="bank")
            nc.tensor.matmul(
                bank[:, 0:32],
                lhsT=gather[:].rearrange("p b i -> p (b i)"),
                rhs=banks[("kept", h, q)][:].rearrange("p x t -> p (x t)"),
                start=True,
                stop=True,
            )
            part = small.tile([128, 2, 16], F32, name="part")
            nc.vector.tensor_tensor(
                out=part[:],
                in0=bank[:, 0:32].rearrange("p (j x) -> p j x", j=2),
                in1=block_t[:].rearrange("p b t -> p (b t)").unsqueeze(1).to_broadcast([128, 2, 16]),
                op=ALU.mult,
            )
            nc.vector.tensor_reduce(out=u_col[:, h, 2 * q : 2 * q + 2], in_=part[:], axis=AX.X, op=ALU.add)

        def memory(h, r):
            nt = nrows.tile([128, P], BF16, name="nt")
            n_in[(h, r)] = nt
            rows = slice(r * 128, (r + 1) * 128)
            for c in range(GM):
                cols = slice(c * 512, (c + 1) * 512)
                bank = psum.tile([128, 512], F32, name="bank")
                for g in range(GM):
                    nc.tensor.matmul_mx(
                        out=bank[:],
                        lhsT=m_c[:, h, g, rows].bitcast(FP8X4),
                        lhsT_scale=m_s[:, h, g, rows],
                        rhs=at_c[:, g, cols].bitcast(FP8X4),
                        rhs_scale=at_s[4 * g : 128, cols],
                        start=(g == 0),
                        stop=(g == GM - 1),
                    )
                for u in range(2):
                    lo = c * 512 + u * 256
                    nc.vector.scalar_tensor_tensor(
                        out=nt[:, lo : lo + 256].rearrange("p (x e) -> p x e", e=2),
                        in0=b_all[:, c, u * 256 : (u + 1) * 256].rearrange("p (x e) -> p x e", e=2),
                        scalar=u_col[:, h, r : r + 1],
                        in1=bank[:].rearrange("p (x u e) -> p u x e", u=2, e=2)[:, u],
                        op0=ALU.mult,
                        op1=ALU.add,
                    )

        def turn_n(h, q):
            for g in range(GM):
                banks[("n", h, q, g)] = turn(
                    lambda j, u: n_in[(h, 2 * q + j)][:].bitcast(F32)[:, 256 * g + 128 * u : 256 * g + 128 * (u + 1)]
                )

        def take_n(h, q, copy):
            for g in range(GM):
                take_words(n_g[:, h, g, q * 1024 : (q + 1) * 1024], banks[("n", h, q, g)], copy)

        def quantize_n(h, q):
            for g in range(GM):
                quantize(n_g, n_c, n_s, h, q, g)

        def out_columns(h, r, c):
            width = 256 if (h, r) == (1, 3) else 512
            return width, slice(c * width, (c + 1) * width)

        def start_out(h, r, c):
            width, cols = out_columns(h, r, c)
            rows = slice(r * 128, (r + 1) * 128)
            bank = psum.tile([128, 512], F32, name="bank")
            banks[("out", h, r, c)] = bank
            for g in range(GZ):
                nc.tensor.matmul_mx(
                    out=bank[:, 0:width],
                    lhsT=z_c[:, h, g, rows].bitcast(FP8X4),
                    lhsT_scale=z_s[:, h, g, rows],
                    rhs=wz_c[:, g, cols].bitcast(FP8X4),
                    rhs_scale=wz_s[4 * g : 128, cols],
                    start=(g == 0),
                    stop=False,
                )

        def end_out(h, r, c):
            width, cols = out_columns(h, r, c)
            rows = slice(r * 128, (r + 1) * 128)
            bank = banks[("out", h, r, c)]
            for g in range(GM):
                nc.tensor.matmul_mx(
                    out=bank[:, 0:width],
                    lhsT=n_c[:, h, g, rows].bitcast(FP8X4),
                    lhsT_scale=n_s[:, h, g, rows],
                    rhs=wm_c[:, g, cols].bitcast(FP8X4),
                    rhs_scale=wm_s[4 * g : 128, cols],
                    start=False,
                    stop=(g == GM - 1),
                )
            res = results.tile([128, 512], F32, name="res")
            nc.scalar.activation(out=res[:, 0:width], in_=bank[:, 0:width], func=ACT.Tanh)
            nc.sync.dma_start(out=out_rows[h][:, r, cols], in_=res[:, 0:width])

        nc.vector.memset(table[:], 0.0)
        nc.vector.memset(ones[:], 1.0)
        nc.vector.memset(b_row[:], 0.0)
        for planes in (at_s, wz_s, wm_s):
            nc.vector.memset(planes[:].bitcast(I32), 0)
        make_identity(nc, ident[:])
        nc.scalar.activation(out=table[:], in_=table[:], func=ACT.Tanh)

        load_m(0, 0, 1)
        load_m(0, 1, 2)
        load_z(0, 3)
        load_m(0, 2, 4)
        load_small(m_fac[:], m_scale.rearrange("o (g p t) -> p (o g) t", p=128, t=4))
        load_z(0, 2)
        load_z(1, 2)
        load_z(1, 3)
        load_z(0, 1, 0, 512)
        load_z(0, 0, 512, K)
        load_small(b_row[0:1, :], bvec.rearrange("(o n) -> o n", o=1))
        load_z(0, 1, 512, K)
        load_z(0, 0, 0, 512)
        load_z(1, 0)
        load_z(1, 1)
        load_small(ez_col[:], ez.rearrange("(g p t) -> p g t", p=128, t=4))
        load_words(at_c, at_words, 1)
        load_words(wz_c, wz_words, 0)
        load_m(1, 2, 4)
        load_scales(at_s, at_scales, GM)
        load_words(at_c, at_words, 0)
        load_m(1, 0, 2)
        load_words(wm_c, wm_words, 0)
        load_scales(wz_s, wz_scales, GZ)
        load_words(wz_c, wz_words, 2)
        load_words(wz_c, wz_words, 1)
        load_words(wm_c, wm_words, 1)
        load_scales(wm_s, wm_scales, GM)

        for dummy in range(6):
            keep_busy()
        make_masks()
        widen_m(0, 0, on_vector)
        turn_m(0, 0)
        widen_m(0, 1, on_vector)
        scale_m(0, 0)
        for dummy in range(2):
            keep_busy()
        order_m(0, 1, on_scalar)
        turn_z(0, 1)
        keep_busy()
        order_z(1, 1, on_scalar)
        turn_m(0, 1)
        scale_m(0, 1)
        take_z(0, 1, on_scalar)
        quantize_z(0, 1)
        turn_z(1, 1)
        take_z(1, 1, on_scalar)
        keep_busy()
        turn_z(0, 0)
        take_z(0, 0, on_scalar)
        keep_busy()
        order_z(1, 0, on_vector)
        quantize_z(0, 0)
        keep_busy()
        write_products(0, 1)
        write_products(1, 1)
        spread_b()
        take_b(on_scalar)
        write_products(0, 0)
        widen_m(1, 1, on_vector)
        turn_z(1, 0)
        sum_products(0, 0)
        take_z(1, 0, on_scalar)
        sum_products(0, 1)
        memory(0, 0)
        memory(0, 3)
        memory(0, 1)
        write_products(1, 0)
        widen_m(1, 0, on_scalar)
        order_m(1, 0, on_scalar)
        memory(0, 2)
        turn_n(0, 0)
        sum_products(1, 0)
        sum_products(1, 1)
        order_m(1, 1, on_scalar)
        turn_m(1, 1)
        scale_m(1, 1)
        take_n(0, 0, on_scalar)
        quantize_n(0, 0)
        turn_n(0, 1)
        take_n(0, 1, on_scalar)
        quantize_n(0, 1)
        turn_m(1, 0)
        start_out(0, 0, 0)
        start_out(0, 2, 0)
        start_out(0, 1, 1)
        start_out(0, 0, 1)
        start_out(0, 2, 1)
        start_out(0, 3, 1)
        end_out(0, 0, 0)
        end_out(0, 2, 0)
        end_out(0, 3, 1)
        end_out(0, 2, 1)
        end_out(0, 1, 1)
        end_out(0, 0, 1)
        scale_m(1, 0)
        memory(1, 1)
        memory(1, 0)
        memory(1, 2)
        memory(1, 3)
        start_out(0, 1, 0)
        end_out(0, 1, 0)
        start_out(0, 3, 0)
        end_out(0, 3, 0)
        turn_n(1, 0)
        turn_n(1, 1)
        take_n(1, 1, on_scalar)
        quantize_z(1, 0)
        start_out(1, 1, 1)
        start_out(1, 0, 1)
        start_out(1, 0, 0)
        start_out(1, 1, 0)
        take_n(1, 0, on_vector)
        quantize_n(1, 0)
        end_out(1, 0, 1)
        end_out(1, 1, 0)
        end_out(1, 1, 1)
        end_out(1, 0, 0)
        quantize_n(1, 1)
        quantize_z(1, 1)
        start_out(1, 2, 0)
        start_out(1, 3, 1)
        start_out(1, 3, 3)
        end_out(1, 3, 3)
        end_out(1, 2, 0)
        start_out(1, 2, 1)
        end_out(1, 2, 1)
        end_out(1, 3, 1)
        start_out(1, 3, 2)
        end_out(1, 3, 2)
        start_out(1, 3, 0)
        end_out(1, 3, 0)
